import numpy as np
import ml_dtypes


def mxq(x, axis, fmt="e4m3"):
    dtype, down = {"e4m3": (ml_dtypes.float8_e4m3fn, 7), "e5m2": (ml_dtypes.float8_e5m2, 14)}[fmt]
    v = np.moveaxis(np.asarray(x, np.float32).astype(ml_dtypes.bfloat16).astype(np.float64), axis, -1)
    blocks = v.reshape(v.shape[:-1] + (-1, 32))
    amax = np.abs(blocks).max(-1, keepdims=True)
    byte = np.maximum(np.where(amax > 0, np.frexp(amax)[1] - 1 + 127, 0) - down, 1)
    scale = np.exp2(byte - 127.0)
    codes = (blocks / scale).astype(np.float32).astype(dtype).astype(np.float64)
    return np.moveaxis((codes * scale).reshape(v.shape), -1, axis)


WIDE = False


def mx_kscale(k):
    if not WIDE:
        return np.ones(k)
    levels = np.array([10, -10, 5, -5, 0])
    if k % 512:
        return np.exp2(np.random.permutation(np.resize(levels, k // 32))).repeat(32)
    a = np.empty((k // 512, 16))
    for p in range(k // 512):
        a[p, :8] = np.random.permutation(np.resize(levels, 8))
        for g in range(8):
            far = levels[np.abs(levels - a[p, g]) >= 10]
            a[p, g + 8] = far[np.random.randint(len(far))]
    return np.exp2(a.ravel()).repeat(32)


BF16 = ml_dtypes.bfloat16


def bf(x):
    return np.asarray(x, np.float32).astype(BF16)


def f64(x):
    return np.asarray(x).astype(np.float64)

def planes(Y):
    n, m = Y.shape
    b = f64(bf(Y)).reshape(n // 32, 32, m)
    amax = np.abs(b).max(1)
    byte = np.clip(np.where(amax > 0, np.frexp(amax)[1] - 1 + 127 - 7, 1), 1, 254)
    codes = (b * np.exp2(127.0 - byte)[:, None, :]).reshape(n, m).astype(np.float32).astype(ml_dtypes.float8_e4m3fn).view(np.uint8)
    words = codes.reshape(n // 512, 128, 4, m).transpose(0, 1, 3, 2)
    return np.ascontiguousarray(words), np.ascontiguousarray(byte.astype(np.uint8).reshape(n // 512, 16, m))


B, Q, N, D, P = 2, 512, 1024, 512, 512


def setup_inputs():
    s = mx_kscale(D)
    t = mx_kscale(P)
    u = mx_kscale(D)
    return {
        "dec": bf(np.random.standard_normal((B, Q, D)) * s),
        "wl": bf(np.random.standard_normal((D, P)) / np.sqrt(D) / s[:, None]),
        "bl": bf(0.5 * np.random.standard_normal(P)),
        "pq": bf(np.random.standard_normal((B, Q, P)) * t),
        "pk": bf(np.random.standard_normal((N, P)) / t),
        "cq": bf(np.random.standard_normal((B, Q, D)) * u),
        "ck": bf(np.random.standard_normal((B, N, D)) / u),
    }


def conditional_spatial_query(dec, wl, bl, pq):
    lam = (mxq(f64(dec), 2, "e4m3") @ mxq(f64(wl), 0, "e4m3")) + f64(bl)
    return lam * f64(pq)


def core(dec, wl, bl, pq, pk, cq, ck):
    d = dec.shape[-1]
    n = pk.shape[0]
    sq = conditional_spatial_query(dec, wl, bl, pq)
    spatial = mxq(sq, 2, "e4m3") @ mxq(f64(pk), 1, "e4m3").T
    content = mxq(f64(cq), 2, "e4m3") @ mxq(f64(ck), 2, "e4m3").transpose(0, 2, 1)
    z = (content + spatial) / np.sqrt(2 * d)
    e = np.exp(z - z.max(-1, keepdims=True))
    return n * (e / e.sum(-1, keepdims=True))


def reference(dec, wl, bl, pq, pk, cq, ck):
    R_out = core(dec, wl, bl, pq, pk, cq, ck)
    words, scales = planes(np.moveaxis(R_out, 2, 0).reshape(1024, -1))
    return R_out, words, scales

@@ -1,0 +1,519 @@
+from contextlib import ExitStack
+
+import concourse.mybir as mybir
+from concourse.masks import make_identity
+
+B, Q, N, D = 2, 512, 1024, 512
+FLOPS = 2 * B * Q * D * D + 2 * 2 * B * Q * N * D
+
+F32 = mybir.dt.float32
+BF16 = mybir.dt.bfloat16
+U32 = mybir.dt.uint32
+I32 = mybir.dt.int32
+U8 = mybir.dt.uint8
+FP8X4 = mybir.dt.float8_e4m3fn_x4
+ALU = mybir.AluOpType
+ACT = mybir.ActivationFunctionType
+
+P = 128
+HALF = 512
+TILES = B * Q // P
+CHUNK = 256
+INV_SQRT_2D = 1.0 / 32.0
+WARMUPS = 6
+WORD_GROUPS = ((0, 2), (2, 4), (4, 6), (6, 7), (7, 8))
+SCALE_GROUPS = ((0, 8),)
+
+
+def tile_conditionaldetrspatialquerymap_x1_kernel(tc, dec, wl, bl, pq, pk, cq, ck, out_0, out_1, out_2):
+    nc = tc.nc
+    dec_rows = dec.rearrange("b q d -> (b q) d")
+    pq_rows = pq.rearrange("b q d -> (b q) d")
+    cq_rows = cq.rearrange("b q d -> (b q) d")
+    out_rows = out_0.rearrange("b q n -> (b q) n")
+    key_rows = {"pk": pk, "ck0": ck[0], "ck1": ck[1]}
+
+    with ExitStack() as ctx:
+        keep = ctx.enter_context(tc.tile_pool(name="keep", bufs=1))
+        ring = ctx.enter_context(tc.tile_pool(name="ring", bufs=5))
+        psum = ctx.enter_context(tc.psum_pool(name="psum", bufs=1))
+        ctx.enter_context(tc.manual_schedule())
+
+        def bank(role):
+            return psum.tile([P, HALF], F32, name=role, tag=role)
+
+        ident = keep.tile([P, P], F32, name="ident")
+        zeros = keep.tile([P, P], F32, name="zeros")
+        primer = keep.tile([P, 8], F32, name="primer")
+        nc.vector.memset(zeros[:], 0.0)
+        make_identity(nc, ident[:])
+        nc.scalar.activation(out=primer[:, 0:1], in_=zeros[:, 0:1], func=ACT.Exp)
+
+        wl_raw = keep.tile([P, 4, D], BF16, name="wl_raw")
+        bias = keep.tile([P, 4], BF16, name="bias")
+        q_raw = {}
+        k_raw = {}
+
+        def load_queries(name, rows, j0, count):
+            t = keep.tile([P, count, D], BF16, name="%s_raw%d" % (name, j0))
+            nc.sync.dma_start(out=t[:], in_=rows[P * j0 : P * (j0 + count), :].rearrange("(a p) d -> p a d", p=P))
+            for a in range(count):
+                q_raw[name, j0 + a] = t[:, a, :]
+
+        def load_keys(name, c0, count):
+            t = keep.tile([P, count, 2, D], BF16, name="%s_raw%d" % (name, c0))
+            nc.sync.dma_start(out=t[:], in_=key_rows[name][CHUNK * c0 : CHUNK * (c0 + count), :].rearrange("(c p r) d -> p c r d", r=2, p=P))
+            for c in range(count):
+                k_raw[name, c0 + c] = t[:, c, :, :]
+
+        load_keys("pk", 0, 1)
+        load_queries("cq", cq_rows, 0, 2)
+        load_queries("dec", dec_rows, 0, 2)
+        nc.sync.dma_start(out=wl_raw[:], in_=wl.rearrange("(p j) c -> p j c", j=4))
+        load_keys("ck0", 0, 1)
+        load_keys("pk", 1, 1)
+        load_keys("ck0", 2, 1)
+        load_queries("pq", pq_rows, 0, 1)
+        nc.sync.dma_start(out=bias[:], in_=bl.rearrange("(p t) -> p t", t=4))
+        load_keys("ck0", 1, 1)
+        load_keys("ck0", 3, 1)
+        load_keys("pk", 3, 1)
+        load_queries("pq", pq_rows, 1, 1)
+        load_keys("pk", 2, 1)
+        load_queries("dec", dec_rows, 2, 2)
+        load_queries("cq", cq_rows, 2, 2)
+        load_keys("ck1", 0, 2)
+        load_queries("dec", dec_rows, 4, 2)
+        load_queries("pq", pq_rows, 2, 2)
+        load_queries("pq", pq_rows, 4, 2)
+        load_queries("pq", pq_rows, 6, 2)
+        load_queries("cq", cq_rows, 4, 2)
+        load_queries("dec", dec_rows, 6, 2)
+        load_queries("cq", cq_rows, 6, 2)
+        load_keys("ck1", 2, 2)
+
+        wl_codes = keep.tile([P, D], U32, name="wl_codes", align_bytes=64)
+        wl_scales = keep.tile([P, D], U8, name="wl_scales", align_bytes=64)
+        k_codes = {}
+        k_scales = {}
+        for name in key_rows:
+            for h in range(2):
+                k_codes[name, h] = keep.tile([P, HALF], U32, name="%s_codes%d" % (name, h), align_bytes=64)
+                k_scales[name, h] = keep.tile([P, HALF], U8, name="%s_scales%d" % (name, h), align_bytes=64)
+        p_codes = {}
+        p_scales = {}
+        for j0, j1 in WORD_GROUPS:
+            t = keep.tile([P, 2, P * (j1 - j0)], U32, name="p_codes%d" % j0, align_bytes=64)
+            for j in range(j0, j1):
+                p_codes[j] = (t, j0, j1)
+        for j0, j1 in SCALE_GROUPS:
+            t = keep.tile([P, 2, P * (j1 - j0)], U8, name="p_scales%d" % j0, align_bytes=64)
+            for j in range(j0, j1):
+                p_scales[j] = (t, j0, j1)
+        st = {}
+
+        def warm(target, count):
+            for i in range(count):
+                nc.tensor.matmul(out=target[:, 0:P], lhsT=zeros[:], rhs=zeros[:], start=True, stop=True)
+
+        def turn(target, slot, rows):
+            words = rows.bitcast(F32)
+            for u in range(2):
+                nc.tensor.transpose(target[:, P * (slot + u) : P * (slot + u + 1)], words[:, u : 2 * P : 2], ident[:])
+
+        def copy(engine, out, in_):
+            if engine == "scalar":
+                nc.scalar.copy(out=out, in_=in_)
+            else:
+                nc.vector.tensor_copy(out=out, in_=in_)
+
+        def quantize(codes, scales, values):
+            nc.vector.quantize_mx(out=codes.bitcast(FP8X4), scales=scales, in_=values)
+
+        def mx(out, lhs, rhs, start, stop):
+            nc.tensor.matmul_mx(out=out, lhsT=lhs[0].bitcast(FP8X4), lhsT_scale=lhs[1], rhs=rhs[0].bitcast(FP8X4), rhs_scale=rhs[1], start=start, stop=stop)
+
+        grouped = keep.tile([P, 4 * D], BF16, name="wl_grouped", align_bytes=64)
+
+        def wl_group():
+            nc.vector.tensor_copy(out=grouped[:].rearrange("p (t m j) -> p t m j", t=4, j=4), in_=wl_raw[:].rearrange("p j (m t) -> p t m j", t=4))
+
+        def wl_quant():
+            quantize(wl_codes[:], wl_scales[:], grouped[:])
+
+        def key_turn(name, c, role, warmups=0):
+            t = bank(role)
+            warm(t, warmups)
+            for r in range(2):
+                turn(t, 2 * r, k_raw[name, c][:, r, :])
+            st["kbank", name, c] = t
+
+        def key_copy(name, c, engine="scalar"):
+            g = ring.tile([P, 4 * CHUNK], BF16, name="key_grouped", tag="key_grouped", align_bytes=64, bufs=8)
+            copy(engine, g[:].bitcast(F32).rearrange("p (q r u) -> p q r u", r=2, u=2), st["kbank", name, c][:].rearrange("p (r u q) -> p q r u", r=2, u=2))
+            st["kgrouped", name, c] = g
+
+        def key_quant(name, c):
+            cols = slice(CHUNK * (c % 2), CHUNK * (c % 2 + 1))
+            quantize(k_codes[name, c // 2][:, cols], k_scales[name, c // 2][:, cols], st["kgrouped", name, c][:])
+
+        def x_turn(j, role="x", warmups=0):
+            t = bank(role)
+            warm(t, warmups)
+            turn(t, 0, q_raw["dec", j])
+            turn(t, 2, q_raw["cq", j])
+            st["xbank", j] = t
+
+        def x_copy(j, engine="scalar"):
+            g = ring.tile([P, 8 * P], BF16, name="x_grouped", tag="x_grouped", align_bytes=64)
+            copy(engine, g[:].bitcast(F32).rearrange("p (s q u) -> p s q u", s=2, u=2), st["xbank", j][:].rearrange("p (s u q) -> p s q u", s=2, u=2))
+            st["xgrouped", j] = g
+
+        def x_quant(j):
+            codes = keep.tile([P, 2 * P], U32, name="x_codes%d" % j, align_bytes=64)
+            scales = keep.tile([P, 2 * P], U8, name="x_scales%d" % j, align_bytes=64)
+            quantize(codes[:], scales[:], st["xgrouped", j][:])
+            st["dec", j] = (codes[:, 0:P], scales[:, 0:P])
+            st["cq", j] = (codes[:, P : 2 * P], scales[:, P : 2 * P])
+
+        def y_turn(j, role="y"):
+            t = bank(role)
+            turn(t, 0, q_raw["pq", j])
+            st["ybank", j] = t
+
+        def lam_mm(j, role):
+            t = bank(role)
+            for s in range(4):
+                cols = slice(P * s, P * (s + 1))
+                mx(t[:, cols], (wl_codes[:, cols], wl_scales[:, cols]), st["dec", j], True, True)
+            st["lambank", j] = t
+
+        def lam_bias(j):
+            lam = ring.tile([P, 4 * P], F32, name="lam_sb", tag="lam_sb")
+            for s in range(4):
+                cols = slice(P * s, P * (s + 1))
+                nc.scalar.activation(out=lam[:, cols], in_=st["lambank", j][:, cols], func=ACT.Identity, bias=bias[:, s : s + 1])
+            st["lam", j] = lam
+
+        def sq_mul(j):
+            sq = ring.tile([P, 4 * P], BF16, name="sq", tag="sq", align_bytes=64)
+            nc.vector.tensor_tensor(
+                out=sq[:].rearrange("p (q u e) -> p q u e", u=2, e=2),
+                in0=st["lam", j][:].rearrange("p (u e q) -> p q u e", u=2, e=2),
+                in1=st["ybank", j][:, 0 : 2 * P].bitcast(BF16).rearrange("p (u q e) -> p q u e", u=2, e=2),
+                op=ALU.mult,
+            )
+            st["sq_bf16", j] = sq
+
+        def sq_quant(j):
+            codes = ring.tile([P, P], U32, name="sq_codes", tag="sq_codes", align_bytes=64)
+            scales = ring.tile([P, P], U8, name="sq_scales", tag="sq_scales", align_bytes=64)
+            quantize(codes[:], scales[:], st["sq_bf16", j][:])
+            st["sq", j] = (codes[:], scales[:])
+
+        def z_mm(j, h, role):
+            t = bank(role)
+            ck_name = "ck%d" % (j // 4)
+            mx(t[:], st["cq", j], (k_codes[ck_name, h][:], k_scales[ck_name, h][:]), True, False)
+            mx(t[:], st["sq", j], (k_codes["pk", h][:], k_scales["pk", h][:]), False, True)
+            st["zbank", j, h] = t
+
+        def row_min(j, h):
+            if h == 0:
+                st["neg", j] = ring.tile([P, N], F32, name="neg", tag="neg")
+                st["stats", j] = ring.tile([P, 4, 8], F32, name="stats", tag="stats", bufs=8)
+            stats = st["stats", j]
+            nc.vector.tensor_scalar(
+                out=st["neg", j][:, HALF * h : HALF * (h + 1)],
+                in0=st["zbank", j, h][:],
+                scalar1=-INV_SQRT_2D,
+                scalar2=None if h == 0 else stats[:, 0, 0:1],
+                op0=ALU.mult,
+                op1=ALU.min,
+                accum_out=stats[:, h, 0:1],
+            )
+
+        def exp(j):
+            e = ring.tile([P, N], F32, name="e", tag="e")
+            stats = st["stats", j]
+            nc.scalar.activation(out=e[:], in_=st["neg", j][:], func=ACT.Exp, scale=-1.0, bias=stats[:, 1, 0:1], accum_out=stats[:, 2, 0:1])
+            st["e", j] = e
+
+        def recip(j):
+            stats = st["stats", j]
+            nc.vector.reciprocal(out=stats[:, 3, 0:1], in_=stats[:, 2, 0:1])
+
+        def norm_f32(j, engine, g0, g1):
+            if ("r", j) not in st:
+                st["r", j] = ring.tile([P, N], F32, name="r", tag="r")
+            cols = slice(HALF * g0, HALF * g1)
+            engine.tensor_scalar(out=st["r", j][:, cols], in0=st["e", j][:, cols], scalar1=st["stats", j][:, 3, 0:1], scalar2=float(N), op0=ALU.mult, op1=ALU.mult)
+
+        def store_out(j, g0, g1):
+            cols = slice(HALF * g0, HALF * g1)
+            nc.sync.dma_start(out=out_rows[P * j : P * (j + 1), cols], in_=st["r", j][:, cols])
+
+        def norm_bf16(j, engine, g0, g1):
+            if ("pb", j) not in st:
+                st["pb", j] = ring.tile([P, 2, 2, 2 * P], BF16, name="pb", tag="pb")
+            out = st["pb", j][:, :, g0:g1, :].rearrange("p u g (w e) -> p u (g w) e", e=2)
+            cols = slice(HALF * g0, HALF * g1)
+            if engine == "scalar":
+                nc.scalar.copy(out=out, in_=st["r", j][:, cols].rearrange("p (w u e) -> p u w e", u=2, e=2))
+            else:
+                nc.vector.tensor_scalar(
+                    out=out,
+                    in0=st["e", j][:, cols].rearrange("p (w u e) -> p u w e", u=2, e=2),
+                    scalar1=st["stats", j][:, 3, 0:1],
+                    scalar2=float(N),
+                    op0=ALU.mult,
+                    op1=ALU.mult,
+                )
+
+        def p_turn(j, g0=0, g1=2, role="p"):
+            t = bank(role)
+            for g in range(g0, g1):
+                for u in range(2):
+                    nc.tensor.transpose(t[:, P * (2 * g + u) : P * (2 * g + u + 1)], st["pb", j][:, u, g, :].bitcast(F32), ident[:])
+                st["pbank", j, g] = t
+
+        def p_copy(j, g0=0, g1=2, engine="scalar"):
+            if ("pg", j) not in st:
+                st["pg", j] = ring.tile([P, N], BF16, name="pg", tag="pg", align_bytes=64)
+            copy(
+                engine,
+                st["pg", j][:, HALF * g0 : HALF * g1].bitcast(F32).rearrange("p (g q u) -> p g q u", q=P, u=2),
+                st["pbank", j, g0][:, 2 * P * g0 : 2 * P * g1].rearrange("p (g u q) -> p g q u", q=P, u=2),
+            )
+
+        words_out = out_1.rearrange("g p m t -> p g (m t)").bitcast(I32)
+
+        def p_quant(j, g0=0, g1=2):
+            codes, c0, c1 = p_codes[j]
+            scales, s0, s1 = p_scales[j]
+            for g in range(g0, g1):
+                quantize(codes[:, g, P * (j - c0) : P * (j - c0 + 1)], scales[:, g, P * (j - s0) : P * (j - s0 + 1)], st["pg", j][:, HALF * g : HALF * (g + 1)])
+
+        def store_words(j):
+            codes, c0, c1 = p_codes[j]
+            nc.sync.dma_start(out=words_out[:, :, P * c0 : P * c1], in_=codes[:].bitcast(I32))
+
+        def store_scales(j):
+            scales, s0, s1 = p_scales[j]
+            for quad in range(4):
+                queue = nc.scalar if s1 == TILES and quad % 2 == 0 else nc.sync
+                queue.dma_start(
+                    out=out_2[:, 4 * quad : 4 * quad + 4, P * s0 : P * s1].rearrange("g r m -> r g m").bitcast(I32),
+                    in_=scales[32 * quad : 32 * quad + 4, :, :].bitcast(I32),
+                )
+
+        key_turn("pk", 0, "b0", 6)
+        x_turn(0, "b1", 2)
+        x_turn(1, "b2", 0)
+        x_copy(0, "scalar")
+        wl_group()
+        x_copy(1, "scalar")
+        key_turn("ck0", 0, "b3", 2)
+        key_copy("pk", 0, "scalar")
+        key_turn("pk", 1, "b4", 0)
+        x_quant(0)
+        key_copy("ck0", 0, "scalar")
+        wl_quant()
+        key_turn("ck0", 2, "b5", 0)
+        x_quant(1)
+        lam_mm(0, "b6")
+        key_quant("ck0", 0)
+        key_copy("ck0", 2, "scalar")
+        key_copy("pk", 1, "vector")
+        lam_mm(1, "b7")
+        lam_bias(0)
+        key_turn("ck0", 1, "b1", 0)
+        key_quant("pk", 1)
+        y_turn(0, "b2")
+        key_quant("pk", 0)
+        key_turn("pk", 3, "b0", 1)
+        key_copy("ck0", 1, "scalar")
+        sq_mul(0)
+        key_turn("ck0", 3, "b3", 0)
+        lam_bias(1)
+        key_quant("ck0", 1)
+        y_turn(1, "b5")
+        sq_quant(0)
+        key_copy("pk", 3, "scalar")
+        key_turn("pk", 2, "b4", 1)
+        sq_mul(1)
+        key_copy("ck0", 3, "scalar")
+        z_mm(0, 0, "b6")
+        key_quant("pk", 3)
+        key_copy("pk", 2, "scalar")
+        key_quant("ck0", 2)
+        x_turn(2, "b1", 0)
+        key_quant("ck0", 3)
+        key_quant("pk", 2)
+        x_turn(3, "b2", 0)
+        sq_quant(1)
+        row_min(0, 0)
+        x_copy(2, "scalar")
+        z_mm(0, 1, "b7")
+        x_copy(3, "scalar")
+        x_quant(2)
+        z_mm(1, 0, "b0")
+        row_min(0, 1)
+        lam_mm(2, "b5")
+        z_mm(1, 1, "b3")
+        row_min(1, 0)
+        lam_bias(2)
+        y_turn(2, "b4")
+        x_quant(3)
+        y_turn(3, "b6")
+        row_min(1, 1)
+        exp(0)
+        lam_mm(3, "b1")
+        sq_mul(2)
+        x_turn(4, "b2", 0)
+        lam_bias(3)
+        key_turn("ck1", 0, "b7", 0)
+        recip(0)
+        sq_quant(2)
+        norm_bf16(0, "vector", 0, 2)
+        x_copy(4, "scalar")
+        z_mm(2, 0, "b0")
+        sq_mul(3)
+        norm_f32(0, nc.gpsimd, 0, 2)
+        key_copy("ck1", 0, "scalar")
+        z_mm(2, 1, "b5")
+        row_min(2, 0)
+        exp(1)
+        p_turn(0, 0, 2, "b3")
+        key_quant("ck1", 0)
+        key_turn("ck1", 1, "b4", 0)
+        sq_quant(3)
+        store_out(0, 0, 2)
+        x_quant(4)
+        p_copy(0, 0, 2, "scalar")
+        z_mm(3, 0, "b1")
+        recip(1)
+        row_min(2, 1)
+        key_copy("ck1", 1, "scalar")
+        norm_f32(1, nc.gpsimd, 0, 2)
+        z_mm(3, 1, "b2")
+        row_min(3, 0)
+        exp(2)
+        lam_mm(4, "b6")
+        x_turn(5, "b7", 0)
+        key_quant("ck1", 1)
+        norm_bf16(1, "vector", 0, 2)
+        store_out(1, 0, 2)
+        lam_bias(4)
+        key_turn("ck1", 2, "b0", 0)
+        recip(2)
+        p_quant(0, 0, 2)
+        y_turn(4, "b3")
+        x_copy(5, "scalar")
+        row_min(3, 1)
+        norm_f32(2, nc.gpsimd, 0, 2)
+        key_turn("ck1", 3, "b5", 0)
+        key_copy("ck1", 2, "scalar")
+        sq_mul(4)
+        y_turn(5, "b4")
+        x_turn(6, "b1", 0)
+        key_copy("ck1", 3, "scalar")
+        x_quant(5)
+        p_turn(1, 0, 2, "b6")
+        exp(3)
+        sq_quant(4)
+        store_out(2, 0, 2)
+        key_quant("ck1", 2)
+        lam_mm(5, "b7")
+        key_quant("ck1", 3)
+        z_mm(4, 0, "b2")
+        norm_bf16(2, "vector", 0, 2)
+        lam_bias(5)
+        z_mm(4, 1, "b0")
+        recip(3)
+        row_min(4, 0)
+        norm_f32(3, nc.gpsimd, 0, 2)
+        p_copy(1, 0, 2, "scalar")
+        x_turn(7, "b3", 0)
+        sq_mul(5)
+        x_copy(6, "scalar")
+        y_turn(7, "b5")
+        y_turn(6, "b7")
+        row_min(4, 1)
+        x_copy(7, "scalar")
+        p_turn(2, 0, 2, "b2")
+        store_out(3, 0, 2)
+        sq_quant(5)
+        x_quant(6)
+        exp(4)
+        z_mm(5, 0, "b6")
+        norm_bf16(3, "vector", 0, 2)
+        lam_mm(6, "b4")
+        p_quant(1, 0, 2)
+        z_mm(5, 1, "b1")
+        row_min(5, 0)
+        lam_bias(6)
+        store_words(0)
+        p_turn(3, 0, 2, "b3")
+        recip(4)
+        x_quant(7)
+        row_min(5, 1)
+        norm_f32(4, nc.gpsimd, 0, 2)
+        p_copy(3, 0, 2, "scalar")
+        lam_mm(7, "b0")
+        sq_mul(6)
+        exp(5)
+        sq_quant(6)
+        store_out(4, 0, 2)
+        norm_bf16(4, "vector", 0, 2)
+        z_mm(6, 0, "b6")
+        lam_bias(7)
+        recip(5)
+        p_quant(3, 0, 2)
+        p_turn(4, 0, 2, "b4")
+        norm_f32(5, nc.gpsimd, 0, 2)
+        row_min(6, 0)
+        z_mm(6, 1, "b1")
+        p_copy(4, 0, 2, "scalar")
+        sq_mul(7)
+        p_copy(2, 0, 2, "scalar")
+        row_min(6, 1)
+        store_out(5, 0, 2)
+        sq_quant(7)
+        norm_bf16(5, "vector", 0, 2)
+        exp(6)
+        z_mm(7, 0, "b3")
+        p_quant(2, 0, 2)
+        z_mm(7, 1, "b7")
+        row_min(7, 0)
+        store_words(2)
+        p_turn(5, 0, 2, "b0")
+        recip(6)
+        p_quant(4, 0, 2)
+        p_copy(5, 0, 2, "scalar")
+        row_min(7, 1)
+        norm_f32(6, nc.gpsimd, 0, 2)
+        exp(7)
+        norm_bf16(6, "vector", 0, 2)
+        store_out(6, 0, 2)
+        p_quant(5, 0, 2)
+        p_turn(6, 0, 2, "b6")
+        recip(7)
+        store_words(4)
+        norm_bf16(7, "vector", 1, 2)
+        p_copy(6, 0, 2, "scalar")
+        norm_bf16(7, "vector", 0, 1)
+        norm_f32(7, nc.vector, 1, 2)
+        p_turn(7, 0, 1, "b4")
+        norm_f32(7, nc.vector, 0, 1)
+        p_turn(7, 1, 2, "b5")
+        store_out(7, 1, 2)
+        p_quant(6, 0, 2)
+        p_copy(7, 0, 1, "scalar")
+        p_copy(7, 1, 2, "scalar")
+        store_words(6)
+        p_quant(7, 0, 1)
+        store_out(7, 0, 1)
+        p_quant(7, 1, 2)
+        store_words(7)
+        store_scales(6)

@@ -16,504 +16,419 @@ ALU = mybir.AluOpType
 ACT = mybir.ActivationFunctionType
 
 P = 128
+ROWS = 256
 HALF = 512
+CHUNKS = B * Q // ROWS
 TILES = B * Q // P
-CHUNK = 256
-INV_SQRT_2D = 1.0 / 32.0
-WARMUPS = 6
-WORD_GROUPS = ((0, 2), (2, 4), (4, 6), (6, 7), (7, 8))
-SCALE_GROUPS = ((0, 8),)
+KEY_CHUNKS = N // ROWS
+NG = 6
+HS = (4, 5, 6)
 
 
 def tile_conditionaldetrspatialquerymap_x1_kernel(tc, dec, wl, bl, pq, pk, cq, ck, out_0, out_1, out_2):
     nc = tc.nc
-    dec_rows = dec.rearrange("b q d -> (b q) d")
-    pq_rows = pq.rearrange("b q d -> (b q) d")
-    cq_rows = cq.rearrange("b q d -> (b q) d")
-    out_rows = out_0.rearrange("b q n -> (b q) n")
-    key_rows = {"pk": pk, "ck0": ck[0], "ck1": ck[1]}
-
     with ExitStack() as ctx:
-        keep = ctx.enter_context(tc.tile_pool(name="keep", bufs=1))
-        ring = ctx.enter_context(tc.tile_pool(name="ring", bufs=5))
-        psum = ctx.enter_context(tc.psum_pool(name="psum", bufs=1))
+        sb = ctx.enter_context(tc.tile_pool(name="sb", bufs=1))
+        ps = ctx.enter_context(tc.psum_pool(name="ps", bufs=1))
         ctx.enter_context(tc.manual_schedule())
 
-        def bank(role):
-            return psum.tile([P, HALF], F32, name=role, tag=role)
+        def tiles(name, count, shape, dtype):
+            return [sb.tile(shape, dtype, name="%s%d" % (name, i), align_bytes=64) for i in range(count)]
 
-        ident = keep.tile([P, P], F32, name="ident")
-        zeros = keep.tile([P, P], F32, name="zeros")
-        primer = keep.tile([P, 8], F32, name="primer")
-        nc.vector.memset(zeros[:], 0.0)
+        banks = [ps.tile([P, HALF], F32, name="bank%d" % i) for i in range(8)]
+        ident = sb.tile([P, P], F32, name="ident")
         make_identity(nc, ident[:])
-        nc.scalar.activation(out=primer[:, 0:1], in_=zeros[:, 0:1], func=ACT.Exp)
 
-        wl_raw = keep.tile([P, 4, D], BF16, name="wl_raw")
-        bias = keep.tile([P, 4], BF16, name="bias")
-        q_raw = {}
-        k_raw = {}
+        dec2 = dec.rearrange("b q k -> (b q) k")
+        pq2 = pq.rearrange("b q k -> (b q) k")
+        cq2 = cq.rearrange("b q k -> (b q) k")
+        ck2 = ck.rearrange("b n k -> (b n) k")
+        out_rows = out_0.rearrange("b q n -> (b q) n")
+        out_words = out_1.rearrange("g p m t -> p g (m t)").bitcast(I32)
+        out_scales = out_2.bitcast(I32)
+        source = {"dec": dec2, "pq": pq2, "cq": cq2, "ck": ck2, "pk": pk}
+        count = {"dec": CHUNKS, "pq": CHUNKS, "cq": CHUNKS, "ck": B * KEY_CHUNKS, "pk": KEY_CHUNKS}
+        raw = {name: tiles(name + "_raw", count[name], [P, 2, D], BF16) for name in source}
+        width = {"dec": ROWS, "cq": ROWS, "sq": ROWS, "ck": HALF, "pk": HALF}
+        operands = {"dec": CHUNKS, "cq": CHUNKS, "sq": CHUNKS, "ck": B * N // HALF, "pk": N // HALF}
+        codes = {name: tiles(name + "_codes", operands[name], [P, width[name]], U32) for name in width}
+        scales = {name: tiles(name + "_scales", operands[name], [P, width[name]], U8) for name in width}
+        grouped = tiles("grouped", NG, [P, 4 * ROWS], BF16)
+        wl_raw = sb.tile([P, 4, D], BF16, name="wl_raw")
+        wl_grouped = sb.tile([P, 4 * D], BF16, name="wl_grouped", align_bytes=64)
+        wl_codes = sb.tile([P, D], U32, name="wl_codes", align_bytes=64)
+        wl_scales = sb.tile([P, D], U8, name="wl_scales", align_bytes=64)
+        bl_raw = sb.tile([P, 4], BF16, name="bl_raw")
+        bl_f32 = sb.tile([P, 4], F32, name="bl_f32")
+        lam = tiles("lam", 2, [P, 4 * ROWS], F32)
+        sq_grouped = tiles("sq_grouped", 2, [P, 4 * ROWS], BF16)
+        neg_z = tiles("neg_z", 3, [P, N], F32)
+        expz = tiles("expz", 3, [P, N], F32)
+        result = tiles("result", 3, [P, N], F32)
+        result16 = tiles("result16", 2, [P, N], BF16)
+        stats = tiles("stats", TILES, [P, 4], F32)
+        plane_in = tiles("plane_in", 2, [P, 2, 4 * ROWS], BF16)
+        plane_codes = tiles("plane_codes", CHUNKS, [P, 2, ROWS], U32)
+        plane_scales = tiles("plane_scales", B, [P, 2, Q], U8)
 
-        def load_queries(name, rows, j0, count):
-            t = keep.tile([P, count, D], BF16, name="%s_raw%d" % (name, j0))
-            nc.sync.dma_start(out=t[:], in_=rows[P * j0 : P * (j0 + count), :].rearrange("(a p) d -> p a d", p=P))
-            for a in range(count):
-                q_raw[name, j0 + a] = t[:, a, :]
+        def load(name, c):
+            rows = source[name][c * ROWS : (c + 1) * ROWS, :]
+            order = "(r p) k -> p r k" if name == "pq" else "(p r) k -> p r k"
+            nc.sync.dma_start(out=raw[name][c][:], in_=rows.rearrange(order, r=2))
 
-        def load_keys(name, c0, count):
-            t = keep.tile([P, count, 2, D], BF16, name="%s_raw%d" % (name, c0))
-            nc.sync.dma_start(out=t[:], in_=key_rows[name][CHUNK * c0 : CHUNK * (c0 + count), :].rearrange("(c p r) d -> p c r d", r=2, p=P))
-            for c in range(count):
-                k_raw[name, c0 + c] = t[:, c, :, :]
-
-        load_keys("pk", 0, 1)
-        load_queries("cq", cq_rows, 0, 2)
-        load_queries("dec", dec_rows, 0, 2)
-        nc.sync.dma_start(out=wl_raw[:], in_=wl.rearrange("(p j) c -> p j c", j=4))
-        load_keys("ck0", 0, 1)
-        load_keys("pk", 1, 1)
-        load_keys("ck0", 2, 1)
-        load_queries("pq", pq_rows, 0, 1)
-        nc.sync.dma_start(out=bias[:], in_=bl.rearrange("(p t) -> p t", t=4))
-        load_keys("ck0", 1, 1)
-        load_keys("ck0", 3, 1)
-        load_keys("pk", 3, 1)
-        load_queries("pq", pq_rows, 1, 1)
-        load_keys("pk", 2, 1)
-        load_queries("dec", dec_rows, 2, 2)
-        load_queries("cq", cq_rows, 2, 2)
-        load_keys("ck1", 0, 2)
-        load_queries("dec", dec_rows, 4, 2)
-        load_queries("pq", pq_rows, 2, 2)
-        load_queries("pq", pq_rows, 4, 2)
-        load_queries("pq", pq_rows, 6, 2)
-        load_queries("cq", cq_rows, 4, 2)
-        load_queries("dec", dec_rows, 6, 2)
-        load_queries("cq", cq_rows, 6, 2)
-        load_keys("ck1", 2, 2)
-
-        wl_codes = keep.tile([P, D], U32, name="wl_codes", align_bytes=64)
-        wl_scales = keep.tile([P, D], U8, name="wl_scales", align_bytes=64)
-        k_codes = {}
-        k_scales = {}
-        for name in key_rows:
-            for h in range(2):
-                k_codes[name, h] = keep.tile([P, HALF], U32, name="%s_codes%d" % (name, h), align_bytes=64)
-                k_scales[name, h] = keep.tile([P, HALF], U8, name="%s_scales%d" % (name, h), align_bytes=64)
-        p_codes = {}
-        p_scales = {}
-        for j0, j1 in WORD_GROUPS:
-            t = keep.tile([P, 2, P * (j1 - j0)], U32, name="p_codes%d" % j0, align_bytes=64)
-            for j in range(j0, j1):
-                p_codes[j] = (t, j0, j1)
-        for j0, j1 in SCALE_GROUPS:
-            t = keep.tile([P, 2, P * (j1 - j0)], U8, name="p_scales%d" % j0, align_bytes=64)
-            for j in range(j0, j1):
-                p_scales[j] = (t, j0, j1)
-        st = {}
-
-        def warm(target, count):
-            for i in range(count):
-                nc.tensor.matmul(out=target[:, 0:P], lhsT=zeros[:], rhs=zeros[:], start=True, stop=True)
-
-        def turn(target, slot, rows):
-            words = rows.bitcast(F32)
-            for u in range(2):
-                nc.tensor.transpose(target[:, P * (slot + u) : P * (slot + u + 1)], words[:, u : 2 * P : 2], ident[:])
-
-        def copy(engine, out, in_):
-            if engine == "scalar":
-                nc.scalar.copy(out=out, in_=in_)
-            else:
-                nc.vector.tensor_copy(out=out, in_=in_)
-
-        def quantize(codes, scales, values):
-            nc.vector.quantize_mx(out=codes.bitcast(FP8X4), scales=scales, in_=values)
-
-        def mx(out, lhs, rhs, start, stop):
-            nc.tensor.matmul_mx(out=out, lhsT=lhs[0].bitcast(FP8X4), lhsT_scale=lhs[1], rhs=rhs[0].bitcast(FP8X4), rhs_scale=rhs[1], start=start, stop=stop)
-
-        grouped = keep.tile([P, 4 * D], BF16, name="wl_grouped", align_bytes=64)
-
-        def wl_group():
-            nc.vector.tensor_copy(out=grouped[:].rearrange("p (t m j) -> p t m j", t=4, j=4), in_=wl_raw[:].rearrange("p j (m t) -> p t m j", t=4))
-
-        def wl_quant():
-            quantize(wl_codes[:], wl_scales[:], grouped[:])
-
-        def key_turn(name, c, role, warmups=0):
-            t = bank(role)
-            warm(t, warmups)
+        def turn(name, c, bank):
             for r in range(2):
-                turn(t, 2 * r, k_raw[name, c][:, r, :])
-            st["kbank", name, c] = t
+                words = raw[name][c][:, r, :].bitcast(F32)
+                for u in range(2):
+                    nc.tensor.transpose(bank[:, (2 * r + u) * P : (2 * r + u + 1) * P], words[:, u : D // 2 : 2], ident[:])
 
-        def key_copy(name, c, engine="scalar"):
-            g = ring.tile([P, 4 * CHUNK], BF16, name="key_grouped", tag="key_grouped", align_bytes=64, bufs=8)
-            copy(engine, g[:].bitcast(F32).rearrange("p (q r u) -> p q r u", r=2, u=2), st["kbank", name, c][:].rearrange("p (r u q) -> p q r u", r=2, u=2))
-            st["kgrouped", name, c] = g
+        def turn_pq(c, bank):
+            slots = bank[:].rearrange("p (r c u i) -> p r u c i", r=2, u=2, i=4)
+            for r in range(2):
+                words = raw["pq"][c][:, r, :].bitcast(F32)
+                for u in range(2):
+                    nc.tensor.transpose(slots[:, r, u], words[:, u : D // 2 : 2], ident[:])
 
-        def key_quant(name, c):
-            cols = slice(CHUNK * (c % 2), CHUNK * (c % 2 + 1))
-            quantize(k_codes[name, c // 2][:, cols], k_scales[name, c // 2][:, cols], st["kgrouped", name, c][:])
+        def gather(bank, dst, on_vector=False):
+            out = dst[:].bitcast(F32).rearrange("p (j r u) -> p j r u", r=2, u=2)
+            in_ = bank[:].rearrange("p (r u j) -> p j r u", r=2, u=2)
+            if on_vector:
+                nc.vector.tensor_copy(out=out, in_=in_)
+            else:
+                nc.scalar.copy(out=out, in_=in_)
 
-        def x_turn(j, role="x", warmups=0):
-            t = bank(role)
-            warm(t, warmups)
-            turn(t, 0, q_raw["dec", j])
-            turn(t, 2, q_raw["cq", j])
-            st["xbank", j] = t
+        def quantize(name, c, src):
+            per = width[name] // ROWS
+            cols = slice((c % per) * ROWS, (c % per + 1) * ROWS)
+            nc.vector.quantize_mx(
+                out=codes[name][c // per][:, cols].bitcast(FP8X4), scales=scales[name][c // per][:, cols], in_=src[:]
+            )
 
-        def x_copy(j, engine="scalar"):
-            g = ring.tile([P, 8 * P], BF16, name="x_grouped", tag="x_grouped", align_bytes=64)
-            copy(engine, g[:].bitcast(F32).rearrange("p (s q u) -> p s q u", s=2, u=2), st["xbank", j][:].rearrange("p (s u q) -> p s q u", s=2, u=2))
-            st["xgrouped", j] = g
+        def group_wl():
+            nc.vector.tensor_copy(
+                out=wl_grouped[:].rearrange("p (t c i j) -> p c t i j", t=4, i=2, j=4),
+                in_=wl_raw[:].rearrange("p j (c i t) -> p c t i j", i=2, t=4),
+            )
 
-        def x_quant(j):
-            codes = keep.tile([P, 2 * P], U32, name="x_codes%d" % j, align_bytes=64)
-            scales = keep.tile([P, 2 * P], U8, name="x_scales%d" % j, align_bytes=64)
-            quantize(codes[:], scales[:], st["xgrouped", j][:])
-            st["dec", j] = (codes[:, 0:P], scales[:, 0:P])
-            st["cq", j] = (codes[:, P : 2 * P], scales[:, P : 2 * P])
+        def quantize_wl():
+            nc.vector.quantize_mx(out=wl_codes[:].bitcast(FP8X4), scales=wl_scales[:], in_=wl_grouped[:])
 
-        def y_turn(j, role="y"):
-            t = bank(role)
-            turn(t, 0, q_raw["pq", j])
-            st["ybank", j] = t
+        def lam_matmul(c, pair, bank):
+            for e in range(2):
+                t = 2 * pair + e
+                nc.tensor.matmul_mx(
+                    out=bank[:, e * ROWS : (e + 1) * ROWS],
+                    lhsT=wl_codes[:, t * P : (t + 1) * P].bitcast(FP8X4),
+                    lhsT_scale=wl_scales[:, t * P : (t + 1) * P],
+                    rhs=codes["dec"][c][:].bitcast(FP8X4),
+                    rhs_scale=scales["dec"][c][:],
+                    start=True,
+                    stop=True,
+                )
 
-        def lam_mm(j, role):
-            t = bank(role)
-            for s in range(4):
-                cols = slice(P * s, P * (s + 1))
-                mx(t[:, cols], (wl_codes[:, cols], wl_scales[:, cols]), st["dec", j], True, True)
-            st["lambank", j] = t
+        def add_bias(c, pair, bank):
+            slots = lam[c % 2][:].rearrange("p (c t i) -> p t c i", t=4, i=4)
+            for e in range(2):
+                t = 2 * pair + e
+                nc.scalar.activation(
+                    out=slots[:, t],
+                    in_=bank[:, e * ROWS : (e + 1) * ROWS].rearrange("p (c i) -> p c i", i=4),
+                    func=ACT.Identity,
+                    bias=bl_f32[:, t : t + 1],
+                )
 
-        def lam_bias(j):
-            lam = ring.tile([P, 4 * P], F32, name="lam_sb", tag="lam_sb")
-            for s in range(4):
-                cols = slice(P * s, P * (s + 1))
-                nc.scalar.activation(out=lam[:, cols], in_=st["lambank", j][:, cols], func=ACT.Identity, bias=bias[:, s : s + 1])
-            st["lam", j] = lam
-
-        def sq_mul(j):
-            sq = ring.tile([P, 4 * P], BF16, name="sq", tag="sq", align_bytes=64)
+        def spatial_query(c, bank):
             nc.vector.tensor_tensor(
-                out=sq[:].rearrange("p (q u e) -> p q u e", u=2, e=2),
-                in0=st["lam", j][:].rearrange("p (u e q) -> p q u e", u=2, e=2),
-                in1=st["ybank", j][:, 0 : 2 * P].bitcast(BF16).rearrange("p (u q e) -> p q u e", u=2, e=2),
+                out=sq_grouped[c % 2][:].rearrange("p (c i u e) -> p c u e i", i=4, u=2, e=2),
+                in0=lam[c % 2][:].rearrange("p (c u e i) -> p c u e i", u=2, e=2, i=4),
+                in1=bank[:].bitcast(BF16).rearrange("p (c u i e) -> p c u e i", u=2, i=4, e=2),
                 op=ALU.mult,
             )
-            st["sq_bf16", j] = sq
 
-        def sq_quant(j):
-            codes = ring.tile([P, P], U32, name="sq_codes", tag="sq_codes", align_bytes=64)
-            scales = ring.tile([P, P], U8, name="sq_scales", tag="sq_scales", align_bytes=64)
-            quantize(codes[:], scales[:], st["sq_bf16", j][:])
-            st["sq", j] = (codes[:], scales[:])
+        def logits(i, h, bank):
+            c, cols = i // 2, slice((i % 2) * P, (i % 2 + 1) * P)
+            b = i * P // Q
+            for first, query, key, k in ((True, "cq", "ck", 2 * b + h), (False, "sq", "pk", h)):
+                nc.tensor.matmul_mx(
+                    out=bank[:],
+                    lhsT=codes[query][c][:, cols].bitcast(FP8X4),
+                    lhsT_scale=scales[query][c][:, cols],
+                    rhs=codes[key][k][:].bitcast(FP8X4),
+                    rhs_scale=scales[key][k][:],
+                    start=first,
+                    stop=not first,
+                )
 
-        def z_mm(j, h, role):
-            t = bank(role)
-            ck_name = "ck%d" % (j // 4)
-            mx(t[:], st["cq", j], (k_codes[ck_name, h][:], k_scales[ck_name, h][:]), True, False)
-            mx(t[:], st["sq", j], (k_codes["pk", h][:], k_scales["pk", h][:]), False, True)
-            st["zbank", j, h] = t
-
-        def row_min(j, h):
-            if h == 0:
-                st["neg", j] = ring.tile([P, N], F32, name="neg", tag="neg")
-                st["stats", j] = ring.tile([P, 4, 8], F32, name="stats", tag="stats", bufs=8)
-            stats = st["stats", j]
+        def scale_and_max(i, h, bank):
             nc.vector.tensor_scalar(
-                out=st["neg", j][:, HALF * h : HALF * (h + 1)],
-                in0=st["zbank", j, h][:],
-                scalar1=-INV_SQRT_2D,
-                scalar2=None if h == 0 else stats[:, 0, 0:1],
+                out=neg_z[i % 3][:, h * HALF : (h + 1) * HALF],
+                in0=bank[:],
+                scalar1=-1.0 / 32.0,
+                scalar2=stats[i][:, 0:1] if h else None,
                 op0=ALU.mult,
                 op1=ALU.min,
-                accum_out=stats[:, h, 0:1],
+                accum_out=stats[i][:, h : h + 1],
             )
 
-        def exp(j):
-            e = ring.tile([P, N], F32, name="e", tag="e")
-            stats = st["stats", j]
-            nc.scalar.activation(out=e[:], in_=st["neg", j][:], func=ACT.Exp, scale=-1.0, bias=stats[:, 1, 0:1], accum_out=stats[:, 2, 0:1])
-            st["e", j] = e
+        def exponentiate(i):
+            nc.scalar.activation(
+                out=expz[i % 3][:], in_=neg_z[i % 3][:], func=ACT.Exp, bias=stats[i][:, 1:2], scale=-1.0,
+                accum_out=stats[i][:, 2:3],
+            )
 
-        def recip(j):
-            stats = st["stats", j]
-            nc.vector.reciprocal(out=stats[:, 3, 0:1], in_=stats[:, 2, 0:1])
+        def invert_sum(i):
+            nc.vector.reciprocal(out=stats[i][:, 3:4], in_=stats[i][:, 2:3])
 
-        def norm_f32(j, engine, g0, g1):
-            if ("r", j) not in st:
-                st["r", j] = ring.tile([P, N], F32, name="r", tag="r")
-            cols = slice(HALF * g0, HALF * g1)
-            engine.tensor_scalar(out=st["r", j][:, cols], in0=st["e", j][:, cols], scalar1=st["stats", j][:, 3, 0:1], scalar2=float(N), op0=ALU.mult, op1=ALU.mult)
+        def normalize(i, engine):
+            engine.tensor_scalar(
+                out=result[i % 3][:], in0=expz[i % 3][:], scalar1=stats[i][:, 3:4], scalar2=float(N),
+                op0=ALU.mult, op1=ALU.mult,
+            )
+            nc.sync.dma_start(out=out_rows[i * P : (i + 1) * P, :], in_=result[i % 3][:])
 
-        def store_out(j, g0, g1):
-            cols = slice(HALF * g0, HALF * g1)
-            nc.sync.dma_start(out=out_rows[P * j : P * (j + 1), cols], in_=st["r", j][:, cols])
-
-        def norm_bf16(j, engine, g0, g1):
-            if ("pb", j) not in st:
-                st["pb", j] = ring.tile([P, 2, 2, 2 * P], BF16, name="pb", tag="pb")
-            out = st["pb", j][:, :, g0:g1, :].rearrange("p u g (w e) -> p u (g w) e", e=2)
-            cols = slice(HALF * g0, HALF * g1)
-            if engine == "scalar":
-                nc.scalar.copy(out=out, in_=st["r", j][:, cols].rearrange("p (w u e) -> p u w e", u=2, e=2))
+        def round_result(i, on_vector=True):
+            out = result16[i % 2][:].rearrange("p (g u m e) -> p g u m e", g=2, u=2, e=2)
+            in_ = result[i % 3][:].rearrange("p (g m u e) -> p g u m e", g=2, u=2, e=2)
+            if on_vector:
+                nc.vector.tensor_copy(out=out, in_=in_)
             else:
-                nc.vector.tensor_scalar(
-                    out=out,
-                    in0=st["e", j][:, cols].rearrange("p (w u e) -> p u w e", u=2, e=2),
-                    scalar1=st["stats", j][:, 3, 0:1],
-                    scalar2=float(N),
-                    op0=ALU.mult,
-                    op1=ALU.mult,
-                )
+                nc.scalar.copy(out=out, in_=in_)
 
-        def p_turn(j, g0=0, g1=2, role="p"):
-            t = bank(role)
-            for g in range(g0, g1):
-                for u in range(2):
-                    nc.tensor.transpose(t[:, P * (2 * g + u) : P * (2 * g + u + 1)], st["pb", j][:, u, g, :].bitcast(F32), ident[:])
-                st["pbank", j, g] = t
+        def turn_result(i, bank):
+            words = result16[i % 2][:].bitcast(F32)
+            for s in range(4):
+                nc.tensor.transpose(bank[:, s * P : (s + 1) * P], words[:, s * P : (s + 1) * P], ident[:])
 
-        def p_copy(j, g0=0, g1=2, engine="scalar"):
-            if ("pg", j) not in st:
-                st["pg", j] = ring.tile([P, N], BF16, name="pg", tag="pg", align_bytes=64)
-            copy(
-                engine,
-                st["pg", j][:, HALF * g0 : HALF * g1].bitcast(F32).rearrange("p (g q u) -> p g q u", q=P, u=2),
-                st["pbank", j, g0][:, 2 * P * g0 : 2 * P * g1].rearrange("p (g u q) -> p g q u", q=P, u=2),
+        def gather_result(i, bank, on_vector=False):
+            dst = plane_in[(i // 2) % 2][:, :, (i % 2) * 4 * P : (i % 2 + 1) * 4 * P].bitcast(F32)
+            out = dst.rearrange("p g (j u) -> p g j u", u=2)
+            in_ = bank[:].rearrange("p (g u j) -> p g j u", g=2, u=2)
+            if on_vector:
+                nc.vector.tensor_copy(out=out, in_=in_)
+            else:
+                nc.scalar.copy(out=out, in_=in_)
+
+        def quantize_result(c, g, lo, hi):
+            b, q0 = c * ROWS // Q, c * ROWS % Q
+            nc.vector.quantize_mx(
+                out=plane_codes[c][:, g, lo:hi].bitcast(FP8X4),
+                scales=plane_scales[b][:, g, q0 + lo : q0 + hi],
+                in_=plane_in[c % 2][:, g, 4 * lo : 4 * hi],
             )
 
-        words_out = out_1.rearrange("g p m t -> p g (m t)").bitcast(I32)
+        def store_words(c, lo, hi):
+            nc.sync.dma_start(
+                out=out_words[:, :, c * ROWS + lo : c * ROWS + hi], in_=plane_codes[c][:, :, lo:hi].bitcast(I32)
+            )
 
-        def p_quant(j, g0=0, g1=2):
-            codes, c0, c1 = p_codes[j]
-            scales, s0, s1 = p_scales[j]
-            for g in range(g0, g1):
-                quantize(codes[:, g, P * (j - c0) : P * (j - c0 + 1)], scales[:, g, P * (j - s0) : P * (j - s0 + 1)], st["pg", j][:, HALF * g : HALF * (g + 1)])
-
-        def store_words(j):
-            codes, c0, c1 = p_codes[j]
-            nc.sync.dma_start(out=words_out[:, :, P * c0 : P * c1], in_=codes[:].bitcast(I32))
-
-        def store_scales(j):
-            scales, s0, s1 = p_scales[j]
+        def store_scales(b, engines):
             for quad in range(4):
-                queue = nc.scalar if s1 == TILES and quad % 2 == 0 else nc.sync
-                queue.dma_start(
-                    out=out_2[:, 4 * quad : 4 * quad + 4, P * s0 : P * s1].rearrange("g r m -> r g m").bitcast(I32),
-                    in_=scales[32 * quad : 32 * quad + 4, :, :].bitcast(I32),
+                engines[quad].dma_start(
+                    out=out_scales[:, 4 * quad : 4 * quad + 4, b * Q // 4 : (b + 1) * Q // 4].rearrange("g r m -> r g m"),
+                    in_=plane_scales[b][32 * quad : 32 * quad + 4].bitcast(I32),
                 )
 
-        key_turn("pk", 0, "b0", 6)
-        x_turn(0, "b1", 2)
-        x_turn(1, "b2", 0)
-        x_copy(0, "scalar")
-        wl_group()
-        x_copy(1, "scalar")
-        key_turn("ck0", 0, "b3", 2)
-        key_copy("pk", 0, "scalar")
-        key_turn("pk", 1, "b4", 0)
-        x_quant(0)
-        key_copy("ck0", 0, "scalar")
-        wl_quant()
-        key_turn("ck0", 2, "b5", 0)
-        x_quant(1)
-        lam_mm(0, "b6")
-        key_quant("ck0", 0)
-        key_copy("ck0", 2, "scalar")
-        key_copy("pk", 1, "vector")
-        lam_mm(1, "b7")
-        lam_bias(0)
-        key_turn("ck0", 1, "b1", 0)
-        key_quant("pk", 1)
-        y_turn(0, "b2")
-        key_quant("pk", 0)
-        key_turn("pk", 3, "b0", 1)
-        key_copy("ck0", 1, "scalar")
-        sq_mul(0)
-        key_turn("ck0", 3, "b3", 0)
-        lam_bias(1)
-        key_quant("ck0", 1)
-        y_turn(1, "b5")
-        sq_quant(0)
-        key_copy("pk", 3, "scalar")
-        key_turn("pk", 2, "b4", 1)
-        sq_mul(1)
-        key_copy("ck0", 3, "scalar")
-        z_mm(0, 0, "b6")
-        key_quant("pk", 3)
-        key_copy("pk", 2, "scalar")
-        key_quant("ck0", 2)
-        x_turn(2, "b1", 0)
-        key_quant("ck0", 3)
-        key_quant("pk", 2)
-        x_turn(3, "b2", 0)
-        sq_quant(1)
-        row_min(0, 0)
-        x_copy(2, "scalar")
-        z_mm(0, 1, "b7")
-        x_copy(3, "scalar")
-        x_quant(2)
-        z_mm(1, 0, "b0")
-        row_min(0, 1)
-        lam_mm(2, "b5")
-        z_mm(1, 1, "b3")
-        row_min(1, 0)
-        lam_bias(2)
-        y_turn(2, "b4")
-        x_quant(3)
-        y_turn(3, "b6")
-        row_min(1, 1)
-        exp(0)
-        lam_mm(3, "b1")
-        sq_mul(2)
-        x_turn(4, "b2", 0)
-        lam_bias(3)
-        key_turn("ck1", 0, "b7", 0)
-        recip(0)
-        sq_quant(2)
-        norm_bf16(0, "vector", 0, 2)
-        x_copy(4, "scalar")
-        z_mm(2, 0, "b0")
-        sq_mul(3)
-        norm_f32(0, nc.gpsimd, 0, 2)
-        key_copy("ck1", 0, "scalar")
-        z_mm(2, 1, "b5")
-        row_min(2, 0)
-        exp(1)
-        p_turn(0, 0, 2, "b3")
-        key_quant("ck1", 0)
-        key_turn("ck1", 1, "b4", 0)
-        sq_quant(3)
-        store_out(0, 0, 2)
-        x_quant(4)
-        p_copy(0, 0, 2, "scalar")
-        z_mm(3, 0, "b1")
-        recip(1)
-        row_min(2, 1)
-        key_copy("ck1", 1, "scalar")
-        norm_f32(1, nc.gpsimd, 0, 2)
-        z_mm(3, 1, "b2")
-        row_min(3, 0)
-        exp(2)
-        lam_mm(4, "b6")
-        x_turn(5, "b7", 0)
-        key_quant("ck1", 1)
-        norm_bf16(1, "vector", 0, 2)
-        store_out(1, 0, 2)
-        lam_bias(4)
-        key_turn("ck1", 2, "b0", 0)
-        recip(2)
-        p_quant(0, 0, 2)
-        y_turn(4, "b3")
-        x_copy(5, "scalar")
-        row_min(3, 1)
-        norm_f32(2, nc.gpsimd, 0, 2)
-        key_turn("ck1", 3, "b5", 0)
-        key_copy("ck1", 2, "scalar")
-        sq_mul(4)
-        y_turn(5, "b4")
-        x_turn(6, "b1", 0)
-        key_copy("ck1", 3, "scalar")
-        x_quant(5)
-        p_turn(1, 0, 2, "b6")
-        exp(3)
-        sq_quant(4)
-        store_out(2, 0, 2)
-        key_quant("ck1", 2)
-        lam_mm(5, "b7")
-        key_quant("ck1", 3)
-        z_mm(4, 0, "b2")
-        norm_bf16(2, "vector", 0, 2)
-        lam_bias(5)
-        z_mm(4, 1, "b0")
-        recip(3)
-        row_min(4, 0)
-        norm_f32(3, nc.gpsimd, 0, 2)
-        p_copy(1, 0, 2, "scalar")
-        x_turn(7, "b3", 0)
-        sq_mul(5)
-        x_copy(6, "scalar")
-        y_turn(7, "b5")
-        y_turn(6, "b7")
-        row_min(4, 1)
-        x_copy(7, "scalar")
-        p_turn(2, 0, 2, "b2")
-        store_out(3, 0, 2)
-        sq_quant(5)
-        x_quant(6)
-        exp(4)
-        z_mm(5, 0, "b6")
-        norm_bf16(3, "vector", 0, 2)
-        lam_mm(6, "b4")
-        p_quant(1, 0, 2)
-        z_mm(5, 1, "b1")
-        row_min(5, 0)
-        lam_bias(6)
-        store_words(0)
-        p_turn(3, 0, 2, "b3")
-        recip(4)
-        x_quant(7)
-        row_min(5, 1)
-        norm_f32(4, nc.gpsimd, 0, 2)
-        p_copy(3, 0, 2, "scalar")
-        lam_mm(7, "b0")
-        sq_mul(6)
-        exp(5)
-        sq_quant(6)
-        store_out(4, 0, 2)
-        norm_bf16(4, "vector", 0, 2)
-        z_mm(6, 0, "b6")
-        lam_bias(7)
-        recip(5)
-        p_quant(3, 0, 2)
-        p_turn(4, 0, 2, "b4")
-        norm_f32(5, nc.gpsimd, 0, 2)
-        row_min(6, 0)
-        z_mm(6, 1, "b1")
-        p_copy(4, 0, 2, "scalar")
-        sq_mul(7)
-        p_copy(2, 0, 2, "scalar")
-        row_min(6, 1)
-        store_out(5, 0, 2)
-        sq_quant(7)
-        norm_bf16(5, "vector", 0, 2)
-        exp(6)
-        z_mm(7, 0, "b3")
-        p_quant(2, 0, 2)
-        z_mm(7, 1, "b7")
-        row_min(7, 0)
-        store_words(2)
-        p_turn(5, 0, 2, "b0")
-        recip(6)
-        p_quant(4, 0, 2)
-        p_copy(5, 0, 2, "scalar")
-        row_min(7, 1)
-        norm_f32(6, nc.gpsimd, 0, 2)
-        exp(7)
-        norm_bf16(6, "vector", 0, 2)
-        store_out(6, 0, 2)
-        p_quant(5, 0, 2)
-        p_turn(6, 0, 2, "b6")
-        recip(7)
-        store_words(4)
-        norm_bf16(7, "vector", 1, 2)
-        p_copy(6, 0, 2, "scalar")
-        norm_bf16(7, "vector", 0, 1)
-        norm_f32(7, nc.vector, 1, 2)
-        p_turn(7, 0, 1, "b4")
-        norm_f32(7, nc.vector, 0, 1)
-        p_turn(7, 1, 2, "b5")
-        store_out(7, 1, 2)
-        p_quant(6, 0, 2)
-        p_copy(7, 0, 1, "scalar")
-        p_copy(7, 1, 2, "scalar")
-        store_words(6)
-        p_quant(7, 0, 1)
-        store_out(7, 0, 1)
-        p_quant(7, 1, 2)
-        store_words(7)
-        store_scales(6)
+        ring = [banks[i] for i in (0, 1, 2, 3, 4, 6, 7)]
+
+        def take():
+            bank = ring.pop(0)
+            ring.append(bank)
+            return bank
+
+        held = {}
+        slot = []
+
+        def T(name, c):
+            if name == "pq":
+                turn_pq(c, banks[5])
+            else:
+                held[name, c] = take()
+                turn(name, c, held[name, c])
+
+        def C(name, c, on_vector=False):
+            slot.append(0)
+            held["g", name, c] = grouped[len(slot) % NG]
+            gather(held[name, c], held["g", name, c], on_vector)
+
+        def Qz(name, c):
+            quantize(name, c, sq_grouped[c % 2] if name == "sq" else held["g", name, c])
+
+        def L(c):
+            for pair in range(2):
+                held["lam", c, pair] = take()
+                lam_matmul(c, pair, held["lam", c, pair])
+
+        def Bi(c, pair):
+            add_bias(c, pair, held["lam", c, pair])
+
+        def M(c):
+            spatial_query(c, banks[5])
+
+        def Z(i, h):
+            logits(i, h, banks[h])
+
+        def Y(i, h):
+            scale_and_max(i, h, banks[h])
+
+        def TO(i):
+            held["o", i] = take()
+            turn_result(i, held["o", i])
+
+        def I(i, on_vector=False):
+            gather_result(i, held["o", i], on_vector)
+
+        def J(i, g):
+            quantize_result(i // 2, g, (i % 2) * P, (i % 2 + 1) * P)
+
+        def Hh(i, g, engine):
+            out = result16[i % 2][:, g * HALF : (g + 1) * HALF].rearrange("p (u m e) -> p u m e", u=2, e=2)
+            in_ = result[i % 3][:, g * HALF : (g + 1) * HALF].rearrange("p (m u e) -> p u m e", u=2, e=2)
+            if engine == "v":
+                nc.vector.tensor_copy(out=out, in_=in_)
+            else:
+                nc.scalar.copy(out=out, in_=in_)
+
+        def He(i, g):
+            nc.vector.tensor_scalar(
+                out=result16[i % 2][:, g * HALF : (g + 1) * HALF].rearrange("p (u m e) -> p u m e", u=2, e=2),
+                in0=expz[i % 3][:, g * HALF : (g + 1) * HALF].rearrange("p (m u e) -> p u m e", u=2, e=2),
+                scalar1=stats[i][:, 3:4], scalar2=float(N), op0=ALU.mult, op1=ALU.mult,
+            )
+
+        def TOh(i, g):
+            held["o", i, g] = take()
+            words = result16[i % 2][:].bitcast(F32)
+            for u in range(2):
+                nc.tensor.transpose(held["o", i, g][:, u * P : (u + 1) * P], words[:, (2 * g + u) * P : (2 * g + u + 1) * P], ident[:])
+
+        def Ih(i, g):
+            dst = plane_in[(i // 2) % 2][:, g, (i % 2) * 4 * P : (i % 2 + 1) * 4 * P].bitcast(F32)
+            nc.vector.tensor_copy(
+                out=dst.rearrange("p (j u) -> p j u", u=2), in_=held["o", i, g][:, 0 : 2 * P].rearrange("p (u j) -> p j u", u=2)
+            )
+
+        def Gs(i, g):
+            cols = slice(g * HALF, (g + 1) * HALF)
+            nc.scalar.activation(out=result[i % 3][:, cols], in_=expz[i % 3][:, cols], func=ACT.Copy, scale=gain[:])
+            nc.sync.dma_start(out=out_rows[i * P : (i + 1) * P, cols], in_=result[i % 3][:, cols])
+
+        gain = sb.tile([P, 1], F32, name="gain")
+
+        nc.sync.dma_start(out=bl_raw[:], in_=bl.rearrange("(p t) -> p t", t=4))
+        load("dec", 0)
+        nc.sync.dma_start(out=wl_raw[:], in_=wl.rearrange("(p j) c -> p j c", j=4))
+        for name, c in (("pk", 0), ("ck", 0), ("pq", 0), ("dec", 1), ("pk", 1), ("ck", 1), ("cq", 0), ("pk", 2), ("ck", 2), ("pk", 3), ("ck", 3), ("pq", 1),
+                        ("cq", 1), ("dec", 2), ("ck", 4), ("pq", 2), ("ck", 5), ("cq", 2), ("dec", 3), ("ck", 6), ("ck", 7), ("pq", 3), ("cq", 3)):
+            load(name, c)
+        nc.scalar.activation(out=bl_f32[:], in_=bl_raw[:], func=ACT.Identity)
+
+        T("dec", 0); C("dec", 0)
+        group_wl()
+        T("pk", 0); C("pk", 0)
+        Qz("dec", 0)
+        quantize_wl()
+        T("ck", 0); C("ck", 0)
+        Qz("pk", 0)
+        T("pq", 0)
+        L(0)
+        T("dec", 1)
+        Qz("ck", 0)
+        Bi(0, 0); Bi(0, 1)
+        C("dec", 1, True)
+        T("pk", 1); C("pk", 1)
+        M(0)
+        ring.remove(banks[0])
+        T("ck", 1); C("ck", 1)
+        T("cq", 0); C("cq", 0)
+        ring.remove(banks[1])
+        Qz("dec", 1); Qz("sq", 0); Qz("pk", 1); Qz("ck", 1)
+        T("pk", 2); C("pk", 2)
+        Qz("cq", 0)
+        T("ck", 2); C("ck", 2)
+        Qz("pk", 2)
+        T("pk", 3); C("pk", 3, True)
+        T("ck", 3); C("ck", 3)
+        Qz("ck", 2)
+        Z(0, 0)
+        L(1)
+        Qz("pk", 3)
+        Qz("ck", 3)
+        Bi(1, 0); Bi(1, 1)
+        Y(0, 0)
+        T("cq", 1); C("cq", 1)
+
+        turns = {0: [("pq", 1), ("dec", 2), ("ck", 4)], 1: [("ck", 5), ("pq", 2), ("cq", 2)], 2: [("dec", 3), ("ck", 6), ("ck", 7)], 3: [("pq", 3), ("cq", 3)]}
+        early = {1: [("ck", 4)], 2: [("cq", 2)], 3: [("ck", 7)], 4: [("cq", 3)]}
+        late = {0: [("dec", 2)], 1: [("ck", 5)], 2: [("dec", 3), ("ck", 6)]}
+        quants = {0: [("cq", 1)], 1: [("ck", 4)], 2: [("ck", 5), ("cq", 2)], 3: [("ck", 6), ("ck", 7)], 4: [("cq", 3)]}
+        quants_late = {0: [("dec", 2)], 2: [("dec", 3)]}
+        LAST = TILES - 1
+        for i in range(LAST):
+            k = i // 2 + 1 if i % 2 == 0 and i < 6 else None
+            Z(i, 1)
+            Z(i + 1, 0)
+            if i in (1, 3):
+                L(i // 2 + 2)
+            if i >= 1:
+                invert_sum(i - 1)
+                normalize(i - 1, nc.gpsimd)
+            for name, c in early.get(i, []):
+                C(name, c)
+            Y(i, 1)
+            exponentiate(i)
+            Y(i + 1, 0)
+            if i in (1, 3):
+                Bi(i // 2 + 2, 0); Bi(i // 2 + 2, 1)
+            if 2 <= i:
+                TO(i - 2)
+            for name, c in turns.get(i, []):
+                T(name, c)
+            if k:
+                M(k)
+            for name, c in late.get(i, [])[:1]:
+                C(name, c)
+            if i in HS:
+                Hh(i - 1, 1, "s")
+            if 2 <= i:
+                I(i - 2)
+            for name, c in late.get(i, [])[1:]:
+                C(name, c)
+            for name, c in quants.get(i, []):
+                Qz(name, c)
+            if 3 <= i:
+                J(i - 3, 0); J(i - 3, 1)
+            if k:
+                Qz("sq", k)
+            if i in HS:
+                Hh(i - 1, 0, "v")
+            elif i >= 1:
+                round_result(i - 1)
+            for name, c in quants_late.get(i, []):
+                Qz(name, c)
+            if i == 4:
+                store_words(0, 0, ROWS)
+            if i == 6:
+                store_words(1, 0, ROWS)
+                store_scales(0, [nc.sync] * 4)
+        Z(7, 1)
+        invert_sum(6)
+        Y(7, 1)
+        exponentiate(7)
+        TO(5); I(5)
+        He(6, 0); He(6, 1)
+        normalize(6, nc.vector)
+        TO(6)
+        J(4, 0); J(4, 1)
+        invert_sum(7)
+        nc.vector.tensor_scalar(out=gain[:], in0=stats[7][:, 3:4], scalar1=float(N), scalar2=None, op0=ALU.mult)
+        He(7, 0); He(7, 1)
+        Gs(7, 0); Gs(7, 1)
+        TOh(7, 0); TOh(7, 1)
+        J(5, 0); J(5, 1)
+        store_words(2, 0, ROWS)
+        I(6)
+        Ih(7, 0); Ih(7, 1)
+        J(7, 0); J(7, 1)
+        J(6, 0); J(6, 1)
+        store_words(3, 0, ROWS)
+        store_scales(1, [nc.scalar, nc.sync, nc.scalar, nc.sync])

@@ -21,8 +21,19 @@ HALF = 512
 CHUNKS = B * Q // ROWS
 TILES = B * Q // P
 KEY_CHUNKS = N // ROWS
-NG = 6
-HS = (4, 5, 6)
+W0, W1, W2 = 10, 1, 1
+HS = (5, 6)
+HF = (2, 4)
+JJ = {4: 0, 6: 1}
+TN = {2: 2}
+CN = {2: 2}
+first = {}
+turns = {0: [("ck", 4), ("ck", 5)], 1: [("pq", 2), ("cq", 2)], 2: [("dec", 3), ("ck", 6), ("ck", 7)], 3: [("pq", 3), ("cq", 3)]}
+early = {1: [("ck", 5)], 2: [("cq", 2)], 3: [("ck", 7)], 4: [("cq", 3)]}
+late = {0: [("ck", 4)], 2: [("dec", 3), ("ck", 6)]}
+mid = {}
+quants = {0: [("cq", 1, 1)], 1: [("ck", 4, 2)], 2: [("cq", 2, 1)], 3: [("ck", 6, 2)], 4: [("cq", 3, 1)]}
+quants_late = {0: [("dec", 2, 1)], 2: [("dec", 3, 1)]}
 
 
 def tile_conditionaldetrspatialquerymap_x1_kernel(tc, dec, wl, bl, pq, pk, cq, ck, out_0, out_1, out_2):
@@ -53,7 +64,7 @@ def tile_conditionaldetrspatialquerymap_x1_kernel(tc, dec, wl, bl, pq, pk, cq, c
         operands = {"dec": CHUNKS, "cq": CHUNKS, "sq": CHUNKS, "ck": B * N // HALF, "pk": N // HALF}
         codes = {name: tiles(name + "_codes", operands[name], [P, width[name]], U32) for name in width}
         scales = {name: tiles(name + "_scales", operands[name], [P, width[name]], U8) for name in width}
-        grouped = tiles("grouped", NG, [P, 4 * ROWS], BF16)
+        grouped = {name: tiles(name + "_grouped", operands[name], [P, 4 * width[name]], BF16) for name in width}
         wl_raw = sb.tile([P, 4, D], BF16, name="wl_raw")
         wl_grouped = sb.tile([P, 4 * D], BF16, name="wl_grouped", align_bytes=64)
         wl_codes = sb.tile([P, D], U32, name="wl_codes", align_bytes=64)
@@ -61,7 +72,6 @@ def tile_conditionaldetrspatialquerymap_x1_kernel(tc, dec, wl, bl, pq, pk, cq, c
         bl_raw = sb.tile([P, 4], BF16, name="bl_raw")
         bl_f32 = sb.tile([P, 4], F32, name="bl_f32")
         lam = tiles("lam", 2, [P, 4 * ROWS], F32)
-        sq_grouped = tiles("sq_grouped", 2, [P, 4 * ROWS], BF16)
         neg_z = tiles("neg_z", 3, [P, N], F32)
         expz = tiles("expz", 3, [P, N], F32)
         result = tiles("result", 3, [P, N], F32)
@@ -90,18 +100,20 @@ def tile_conditionaldetrspatialquerymap_x1_kernel(tc, dec, wl, bl, pq, pk, cq, c
                     nc.tensor.transpose(slots[:, r, u], words[:, u : D // 2 : 2], ident[:])
 
         def gather(bank, dst, on_vector=False):
-            out = dst[:].bitcast(F32).rearrange("p (j r u) -> p j r u", r=2, u=2)
+            out = dst.bitcast(F32).rearrange("p (j r u) -> p j r u", r=2, u=2)
             in_ = bank[:].rearrange("p (r u j) -> p j r u", r=2, u=2)
             if on_vector:
                 nc.vector.tensor_copy(out=out, in_=in_)
             else:
                 nc.scalar.copy(out=out, in_=in_)
 
-        def quantize(name, c, src):
+        def quantize(name, c, chunks=1):
             per = width[name] // ROWS
-            cols = slice((c % per) * ROWS, (c % per + 1) * ROWS)
+            lo, hi = (c % per) * ROWS, (c % per + chunks) * ROWS
             nc.vector.quantize_mx(
-                out=codes[name][c // per][:, cols].bitcast(FP8X4), scales=scales[name][c // per][:, cols], in_=src[:]
+                out=codes[name][c // per][:, lo:hi].bitcast(FP8X4),
+                scales=scales[name][c // per][:, lo:hi],
+                in_=grouped[name][c // per][:, 4 * lo : 4 * hi],
             )
 
         def group_wl():
@@ -139,7 +151,7 @@ def tile_conditionaldetrspatialquerymap_x1_kernel(tc, dec, wl, bl, pq, pk, cq, c
 
         def spatial_query(c, bank):
             nc.vector.tensor_tensor(
-                out=sq_grouped[c % 2][:].rearrange("p (c i u e) -> p c u e i", i=4, u=2, e=2),
+                out=grouped["sq"][c][:].rearrange("p (c i u e) -> p c u e i", i=4, u=2, e=2),
                 in0=lam[c % 2][:].rearrange("p (c u e i) -> p c u e i", u=2, e=2, i=4),
                 in1=bank[:].bitcast(BF16).rearrange("p (c u i e) -> p c u e i", u=2, i=4, e=2),
                 op=ALU.mult,
@@ -209,23 +221,26 @@ def tile_conditionaldetrspatialquerymap_x1_kernel(tc, dec, wl, bl, pq, pk, cq, c
                 nc.scalar.copy(out=out, in_=in_)
 
         def quantize_result(c, g, lo, hi):
-            b, q0 = c * ROWS // Q, c * ROWS % Q
             nc.vector.quantize_mx(
                 out=plane_codes[c][:, g, lo:hi].bitcast(FP8X4),
-                scales=plane_scales[b][:, g, q0 + lo : q0 + hi],
+                scales=plane_scales[c // 2][:, g, (c % 2) * ROWS + lo : (c % 2) * ROWS + hi],
                 in_=plane_in[c % 2][:, g, 4 * lo : 4 * hi],
             )
+
+        def quantize_pair(c):
+            quantize_result(c, 0, 0, ROWS)
+            quantize_result(c, 1, 0, ROWS)
 
         def store_words(c, lo, hi):
             nc.sync.dma_start(
                 out=out_words[:, :, c * ROWS + lo : c * ROWS + hi], in_=plane_codes[c][:, :, lo:hi].bitcast(I32)
             )
 
-        def store_scales(b, engines):
+        def store_scales(c, engines):
             for quad in range(4):
                 engines[quad].dma_start(
-                    out=out_scales[:, 4 * quad : 4 * quad + 4, b * Q // 4 : (b + 1) * Q // 4].rearrange("g r m -> r g m"),
-                    in_=plane_scales[b][32 * quad : 32 * quad + 4].bitcast(I32),
+                    out=out_scales[:, 4 * quad : 4 * quad + 4, c * Q // 4 : (c + 1) * Q // 4].rearrange("g r m -> r g m"),
+                    in_=plane_scales[c][32 * quad : 32 * quad + 4].bitcast(I32),
                 )
 
         ring = [banks[i] for i in (0, 1, 2, 3, 4, 6, 7)]
@@ -236,7 +251,6 @@ def tile_conditionaldetrspatialquerymap_x1_kernel(tc, dec, wl, bl, pq, pk, cq, c
             return bank
 
         held = {}
-        slot = []
 
         def T(name, c):
             if name == "pq":
@@ -246,12 +260,11 @@ def tile_conditionaldetrspatialquerymap_x1_kernel(tc, dec, wl, bl, pq, pk, cq, c
                 turn(name, c, held[name, c])
 
         def C(name, c, on_vector=False):
-            slot.append(0)
-            held["g", name, c] = grouped[len(slot) % NG]
-            gather(held[name, c], held["g", name, c], on_vector)
+            per = width[name] // ROWS
+            gather(held[name, c], grouped[name][c // per][:, (c % per) * 4 * ROWS : (c % per + 1) * 4 * ROWS], on_vector)
 
-        def Qz(name, c):
-            quantize(name, c, sq_grouped[c % 2] if name == "sq" else held["g", name, c])
+        def Qz(name, c, chunks=1):
+            quantize(name, c, chunks)
 
         def L(c):
             for pair in range(2):
@@ -314,54 +327,59 @@ def tile_conditionaldetrspatialquerymap_x1_kernel(tc, dec, wl, bl, pq, pk, cq, c
 
         gain = sb.tile([P, 1], F32, name="gain")
 
-        nc.sync.dma_start(out=bl_raw[:], in_=bl.rearrange("(p t) -> p t", t=4))
-        load("dec", 0)
+        def W(n):
+            for rep in range(n):
+                nc.tensor.matmul(ring[0][:, 0:P], ident[:], ident[:], start=True, stop=True)
+
         nc.sync.dma_start(out=wl_raw[:], in_=wl.rearrange("(p j) c -> p j c", j=4))
-        for name, c in (("pk", 0), ("ck", 0), ("pq", 0), ("dec", 1), ("pk", 1), ("ck", 1), ("cq", 0), ("pk", 2), ("ck", 2), ("pk", 3), ("ck", 3), ("pq", 1),
-                        ("cq", 1), ("dec", 2), ("ck", 4), ("pq", 2), ("ck", 5), ("cq", 2), ("dec", 3), ("ck", 6), ("ck", 7), ("pq", 3), ("cq", 3)):
+        load("dec", 0)
+        nc.sync.dma_start(out=bl_raw[:], in_=bl.rearrange("(p t) -> p t", t=4))
+        for name, c in (("pk", 0), ("ck", 0), ("pq", 0), ("dec", 1), ("pk", 1), ("ck", 1), ("cq", 0), ("pk", 2), ("ck", 2), ("pq", 1), ("pk", 3), ("ck", 3), ("cq", 1), ("dec", 2), ("ck", 4), ("ck", 5), ("pq", 2), ("cq", 2), ("dec", 3), ("ck", 6), ("ck", 7), ("pq", 3), ("cq", 3)):
             load(name, c)
         nc.scalar.activation(out=bl_f32[:], in_=bl_raw[:], func=ACT.Identity)
 
-        T("dec", 0); C("dec", 0)
+        W(W0)
         group_wl()
+        T("dec", 0); C("dec", 0)
+        quantize_wl()
         T("pk", 0); C("pk", 0)
         Qz("dec", 0)
-        quantize_wl()
-        T("ck", 0); C("ck", 0)
+        W(W1)
+        T("ck", 0)
         Qz("pk", 0)
-        T("pq", 0)
+        C("ck", 0, True)
         L(0)
-        T("dec", 1)
-        Qz("ck", 0)
+        T("pq", 0)
         Bi(0, 0); Bi(0, 1)
-        C("dec", 1, True)
+        Qz("ck", 0)
+        T("dec", 1); C("dec", 1)
         T("pk", 1); C("pk", 1)
-        M(0)
         ring.remove(banks[0])
+        W(W2)
+        M(0)
         T("ck", 1); C("ck", 1)
         T("cq", 0); C("cq", 0)
-        ring.remove(banks[1])
         Qz("dec", 1); Qz("sq", 0); Qz("pk", 1); Qz("ck", 1)
         T("pk", 2); C("pk", 2)
-        Qz("cq", 0)
-        T("ck", 2); C("ck", 2)
-        Qz("pk", 2)
-        T("pk", 3); C("pk", 3, True)
-        T("ck", 3); C("ck", 3)
-        Qz("ck", 2)
-        Z(0, 0)
+        ring.remove(banks[1])
         L(1)
+        Bi(1, 0); Bi(1, 1)
+        Qz("cq", 0)
+        Qz("pk", 2)
+        T("ck", 2); C("ck", 2, True)
+        T("pq", 1)
+        T("pk", 3); C("pk", 3)
+        T("ck", 3); C("ck", 3)
+        Z(0, 0)
+        T("cq", 1); C("cq", 1)
+        T("dec", 2); C("dec", 2)
+        M(1)
+        Qz("ck", 2)
         Qz("pk", 3)
         Qz("ck", 3)
-        Bi(1, 0); Bi(1, 1)
         Y(0, 0)
-        T("cq", 1); C("cq", 1)
+        Qz("sq", 1)
 
-        turns = {0: [("pq", 1), ("dec", 2), ("ck", 4)], 1: [("ck", 5), ("pq", 2), ("cq", 2)], 2: [("dec", 3), ("ck", 6), ("ck", 7)], 3: [("pq", 3), ("cq", 3)]}
-        early = {1: [("ck", 4)], 2: [("cq", 2)], 3: [("ck", 7)], 4: [("cq", 3)]}
-        late = {0: [("dec", 2)], 1: [("ck", 5)], 2: [("dec", 3), ("ck", 6)]}
-        quants = {0: [("cq", 1)], 1: [("ck", 4)], 2: [("ck", 5), ("cq", 2)], 3: [("ck", 6), ("ck", 7)], 4: [("cq", 3)]}
-        quants_late = {0: [("dec", 2)], 2: [("dec", 3)]}
         LAST = TILES - 1
         for i in range(LAST):
             k = i // 2 + 1 if i % 2 == 0 and i < 6 else None
@@ -371,64 +389,73 @@ def tile_conditionaldetrspatialquerymap_x1_kernel(tc, dec, wl, bl, pq, pk, cq, c
                 L(i // 2 + 2)
             if i >= 1:
                 invert_sum(i - 1)
-                normalize(i - 1, nc.gpsimd)
+            for name, c in first.get(i, []):
+                T(name, c)
             for name, c in early.get(i, []):
                 C(name, c)
             Y(i, 1)
             exponentiate(i)
+            if i >= 1:
+                normalize(i - 1, nc.vector)
+            for name, c, n in mid.get(i, []):
+                Qz(name, c, n)
             Y(i + 1, 0)
             if i in (1, 3):
                 Bi(i // 2 + 2, 0); Bi(i // 2 + 2, 1)
+            for name, c in turns.get(i, [])[:TN.get(i, 0)]:
+                T(name, c)
             if 2 <= i:
                 TO(i - 2)
-            for name, c in turns.get(i, []):
+            for name, c in turns.get(i, [])[TN.get(i, 0):]:
                 T(name, c)
-            if k:
+            if k and i:
                 M(k)
-            for name, c in late.get(i, [])[:1]:
+            for name, c in late.get(i, [])[:CN.get(i, 1)]:
                 C(name, c)
             if i in HS:
                 Hh(i - 1, 1, "s")
+            if i in HF:
+                round_result(i - 1, False)
             if 2 <= i:
                 I(i - 2)
-            for name, c in late.get(i, [])[1:]:
+            for name, c in late.get(i, [])[CN.get(i, 1):]:
                 C(name, c)
-            for name, c in quants.get(i, []):
-                Qz(name, c)
-            if 3 <= i:
-                J(i - 3, 0); J(i - 3, 1)
-            if k:
+            for name, c, n in quants.get(i, []):
+                Qz(name, c, n)
+            if k and i:
                 Qz("sq", k)
+            if i in JJ:
+                quantize_pair(JJ[i])
             if i in HS:
                 Hh(i - 1, 0, "v")
-            elif i >= 1:
+            elif i >= 1 and i not in HF:
                 round_result(i - 1)
-            for name, c in quants_late.get(i, []):
-                Qz(name, c)
-            if i == 4:
-                store_words(0, 0, ROWS)
-            if i == 6:
-                store_words(1, 0, ROWS)
-                store_scales(0, [nc.sync] * 4)
+            for name, c, n in quants_late.get(i, []):
+                Qz(name, c, n)
+            if i in JJ:
+                store_words(JJ[i], 0, ROWS)
+                if JJ[i] == 1:
+                    store_scales(0, [nc.sync] * 4)
+
         Z(7, 1)
+        TO(5)
         invert_sum(6)
+        I(5)
         Y(7, 1)
         exponentiate(7)
-        TO(5); I(5)
         He(6, 0); He(6, 1)
         normalize(6, nc.vector)
-        TO(6)
-        J(4, 0); J(4, 1)
+        TO(6); I(6)
+        quantize_pair(2)
+        store_words(2, 0, ROWS)
         invert_sum(7)
         nc.vector.tensor_scalar(out=gain[:], in0=stats[7][:, 3:4], scalar1=float(N), scalar2=None, op0=ALU.mult)
         He(7, 0); He(7, 1)
         Gs(7, 0); Gs(7, 1)
         TOh(7, 0); TOh(7, 1)
-        J(5, 0); J(5, 1)
-        store_words(2, 0, ROWS)
-        I(6)
+        J(6, 0); J(6, 1)
+        store_words(3, 0, P)
         Ih(7, 0); Ih(7, 1)
         J(7, 0); J(7, 1)
-        J(6, 0); J(6, 1)
-        store_words(3, 0, ROWS)
+        store_words(3, P, ROWS)
         store_scales(1, [nc.scalar, nc.sync, nc.scalar, nc.sync])

@@ -20,20 +20,16 @@ ROWS = 256
 HALF = 512
 CHUNKS = B * Q // ROWS
 TILES = B * Q // P
-KEY_CHUNKS = N // ROWS
-W0, W1, W2 = 10, 1, 1
-HS = (5, 6)
-HF = (2, 4)
-JJ = {4: 0, 6: 1}
-TN = {2: 2}
-CN = {2: 2}
-first = {}
-turns = {0: [("ck", 4), ("ck", 5)], 1: [("pq", 2), ("cq", 2)], 2: [("dec", 3), ("ck", 6), ("ck", 7)], 3: [("pq", 3), ("cq", 3)]}
-early = {1: [("ck", 5)], 2: [("cq", 2)], 3: [("ck", 7)], 4: [("cq", 3)]}
-late = {0: [("ck", 4)], 2: [("dec", 3), ("ck", 6)]}
-mid = {}
-quants = {0: [("cq", 1, 1)], 1: [("ck", 4, 2)], 2: [("cq", 2, 1)], 3: [("ck", 6, 2)], 4: [("cq", 3, 1)]}
-quants_late = {0: [("dec", 2, 1)], 2: [("dec", 3, 1)]}
+LAST = TILES - 1
+DEPTH = 3
+LOGIT_SCALE = 1.0 / 32.0
+
+WARM_AT_START = 7
+WARM_BEFORE_LAM = 2
+
+LATER_CHUNKS = (("ck", 4), ("ck", 5), ("pq", 2), ("cq", 2), ("dec", 3), ("ck", 6), ("ck", 7), ("pq", 3), ("cq", 3))
+TURNS_PER_STEP = (2, 2, 3, 2)
+SCALAR_ROUNDS = len(TURNS_PER_STEP)
 
 
 def tile_conditionaldetrspatialquerymap_x1_kernel(tc, dec, wl, bl, pq, pk, cq, ck, out_0, out_1, out_2):
@@ -50,16 +46,18 @@ def tile_conditionaldetrspatialquerymap_x1_kernel(tc, dec, wl, bl, pq, pk, cq, c
         ident = sb.tile([P, P], F32, name="ident")
         make_identity(nc, ident[:])
 
-        dec2 = dec.rearrange("b q k -> (b q) k")
-        pq2 = pq.rearrange("b q k -> (b q) k")
-        cq2 = cq.rearrange("b q k -> (b q) k")
-        ck2 = ck.rearrange("b n k -> (b n) k")
+        source = {
+            "dec": dec.rearrange("b q k -> (b q) k"),
+            "pq": pq.rearrange("b q k -> (b q) k"),
+            "cq": cq.rearrange("b q k -> (b q) k"),
+            "ck": ck.rearrange("b n k -> (b n) k"),
+            "pk": pk,
+        }
         out_rows = out_0.rearrange("b q n -> (b q) n")
         out_words = out_1.rearrange("g p m t -> p g (m t)").bitcast(I32)
         out_scales = out_2.bitcast(I32)
-        source = {"dec": dec2, "pq": pq2, "cq": cq2, "ck": ck2, "pk": pk}
-        count = {"dec": CHUNKS, "pq": CHUNKS, "cq": CHUNKS, "ck": B * KEY_CHUNKS, "pk": KEY_CHUNKS}
-        raw = {name: tiles(name + "_raw", count[name], [P, 2, D], BF16) for name in source}
+
+        raw = {name: tiles(name + "_raw", source[name].shape[0] // ROWS, [P, 2, D], BF16) for name in source}
         width = {"dec": ROWS, "cq": ROWS, "sq": ROWS, "ck": HALF, "pk": HALF}
         operands = {"dec": CHUNKS, "cq": CHUNKS, "sq": CHUNKS, "ck": B * N // HALF, "pk": N // HALF}
         codes = {name: tiles(name + "_codes", operands[name], [P, width[name]], U32) for name in width}
@@ -72,40 +70,61 @@ def tile_conditionaldetrspatialquerymap_x1_kernel(tc, dec, wl, bl, pq, pk, cq, c
         bl_raw = sb.tile([P, 4], BF16, name="bl_raw")
         bl_f32 = sb.tile([P, 4], F32, name="bl_f32")
         lam = tiles("lam", 2, [P, 4 * ROWS], F32)
-        neg_z = tiles("neg_z", 3, [P, N], F32)
-        expz = tiles("expz", 3, [P, N], F32)
-        result = tiles("result", 3, [P, N], F32)
+        neg_z = tiles("neg_z", DEPTH, [P, N], F32)
+        exp_z = tiles("exp_z", DEPTH, [P, N], F32)
+        result = tiles("result", DEPTH, [P, N], F32)
         result16 = tiles("result16", 2, [P, N], BF16)
         stats = tiles("stats", TILES, [P, 4], F32)
-        plane_in = tiles("plane_in", 2, [P, 2, 4 * ROWS], BF16)
-        plane_codes = tiles("plane_codes", CHUNKS, [P, 2, ROWS], U32)
-        plane_scales = tiles("plane_scales", B, [P, 2, Q], U8)
+        out_grouped = tiles("out_grouped", 2, [P, 2, 4 * ROWS], BF16)
+        out_codes = tiles("out_codes", CHUNKS, [P, 2, ROWS], U32)
+        out_bytes = tiles("out_bytes", B, [P, 2, Q], U8)
+        warm = sb.tile([P, P], F32, name="warm")
+        nc.vector.memset(warm[:], 0.0)
+        gain = sb.tile([P, 1], F32, name="gain")
+
+        logit_banks = banks[0:2]
+        pq_bank = banks[5]
+        rotation = banks[0:5] + banks[6:8]
+        held = {}
+
+        def take_bank(key):
+            held[key] = rotation.pop(0)
+            rotation.append(held[key])
+            return held[key]
+
+        def warm_up(count):
+            for repeat in range(count):
+                nc.tensor.matmul(rotation[0][:, 0:P], warm[:], warm[:], start=True, stop=True)
 
         def load(name, c):
             rows = source[name][c * ROWS : (c + 1) * ROWS, :]
             order = "(r p) k -> p r k" if name == "pq" else "(p r) k -> p r k"
             nc.sync.dma_start(out=raw[name][c][:], in_=rows.rearrange(order, r=2))
 
-        def turn(name, c, bank):
+        def turn(name, c):
+            if name == "pq":
+                slots = pq_bank[:].rearrange("p (r c u i) -> p r u c i", r=2, u=2, i=4)
+            else:
+                slots = take_bank((name, c))[:].rearrange("p (r u j) -> p r u j", r=2, u=2)
             for r in range(2):
                 words = raw[name][c][:, r, :].bitcast(F32)
                 for u in range(2):
-                    nc.tensor.transpose(bank[:, (2 * r + u) * P : (2 * r + u + 1) * P], words[:, u : D // 2 : 2], ident[:])
-
-        def turn_pq(c, bank):
-            slots = bank[:].rearrange("p (r c u i) -> p r u c i", r=2, u=2, i=4)
-            for r in range(2):
-                words = raw["pq"][c][:, r, :].bitcast(F32)
-                for u in range(2):
                     nc.tensor.transpose(slots[:, r, u], words[:, u : D // 2 : 2], ident[:])
 
-        def gather(bank, dst, on_vector=False):
-            out = dst.bitcast(F32).rearrange("p (j r u) -> p j r u", r=2, u=2)
-            in_ = bank[:].rearrange("p (r u j) -> p j r u", r=2, u=2)
+        def copy(on_vector, out, in_):
             if on_vector:
                 nc.vector.tensor_copy(out=out, in_=in_)
             else:
                 nc.scalar.copy(out=out, in_=in_)
+
+        def gather(name, c, on_vector=False):
+            per = width[name] // ROWS
+            dst = grouped[name][c // per][:, (c % per) * 4 * ROWS : (c % per + 1) * 4 * ROWS].bitcast(F32)
+            copy(
+                on_vector,
+                dst.rearrange("p (j r u) -> p j r u", r=2, u=2),
+                held[name, c][:].rearrange("p (r u j) -> p j r u", r=2, u=2),
+            )
 
         def quantize(name, c, chunks=1):
             per = width[name] // ROWS
@@ -122,14 +141,11 @@ def tile_conditionaldetrspatialquerymap_x1_kernel(tc, dec, wl, bl, pq, pk, cq, c
                 in_=wl_raw[:].rearrange("p j (c i t) -> p c t i j", i=2, t=4),
             )
 
-        def quantize_wl():
-            nc.vector.quantize_mx(out=wl_codes[:].bitcast(FP8X4), scales=wl_scales[:], in_=wl_grouped[:])
-
-        def lam_matmul(c, pair, bank):
-            for e in range(2):
-                t = 2 * pair + e
+        def lam_product(c):
+            for t in range(4):
+                bank = held["lam", t // 2] if t % 2 else take_bank(("lam", t // 2))
                 nc.tensor.matmul_mx(
-                    out=bank[:, e * ROWS : (e + 1) * ROWS],
+                    out=bank[:, (t % 2) * ROWS : (t % 2 + 1) * ROWS],
                     lhsT=wl_codes[:, t * P : (t + 1) * P].bitcast(FP8X4),
                     lhsT_scale=wl_scales[:, t * P : (t + 1) * P],
                     rhs=codes["dec"][c][:].bitcast(FP8X4),
@@ -138,31 +154,30 @@ def tile_conditionaldetrspatialquerymap_x1_kernel(tc, dec, wl, bl, pq, pk, cq, c
                     stop=True,
                 )
 
-        def add_bias(c, pair, bank):
+        def add_bias(c):
             slots = lam[c % 2][:].rearrange("p (c t i) -> p t c i", t=4, i=4)
-            for e in range(2):
-                t = 2 * pair + e
+            for t in range(4):
                 nc.scalar.activation(
                     out=slots[:, t],
-                    in_=bank[:, e * ROWS : (e + 1) * ROWS].rearrange("p (c i) -> p c i", i=4),
+                    in_=held["lam", t // 2][:, (t % 2) * ROWS : (t % 2 + 1) * ROWS].rearrange("p (c i) -> p c i", i=4),
                     func=ACT.Identity,
                     bias=bl_f32[:, t : t + 1],
                 )
 
-        def spatial_query(c, bank):
+        def spatial_query(c):
             nc.vector.tensor_tensor(
                 out=grouped["sq"][c][:].rearrange("p (c i u e) -> p c u e i", i=4, u=2, e=2),
                 in0=lam[c % 2][:].rearrange("p (c u e i) -> p c u e i", u=2, e=2, i=4),
-                in1=bank[:].bitcast(BF16).rearrange("p (c u i e) -> p c u e i", u=2, i=4, e=2),
+                in1=pq_bank[:].bitcast(BF16).rearrange("p (c u i e) -> p c u e i", u=2, i=4, e=2),
                 op=ALU.mult,
             )
 
-        def logits(i, h, bank):
+        def logits(i, h):
             c, cols = i // 2, slice((i % 2) * P, (i % 2 + 1) * P)
             b = i * P // Q
             for first, query, key, k in ((True, "cq", "ck", 2 * b + h), (False, "sq", "pk", h)):
                 nc.tensor.matmul_mx(
-                    out=bank[:],
+                    out=logit_banks[h][:],
                     lhsT=codes[query][c][:, cols].bitcast(FP8X4),
                     lhsT_scale=scales[query][c][:, cols],
                     rhs=codes[key][k][:].bitcast(FP8X4),
@@ -171,11 +186,11 @@ def tile_conditionaldetrspatialquerymap_x1_kernel(tc, dec, wl, bl, pq, pk, cq, c
                     stop=not first,
                 )
 
-        def scale_and_max(i, h, bank):
+        def scale_and_max(i, h):
             nc.vector.tensor_scalar(
-                out=neg_z[i % 3][:, h * HALF : (h + 1) * HALF],
-                in0=bank[:],
-                scalar1=-1.0 / 32.0,
+                out=neg_z[i % DEPTH][:, h * HALF : (h + 1) * HALF],
+                in0=logit_banks[h][:],
+                scalar1=-LOGIT_SCALE,
                 scalar2=stats[i][:, 0:1] if h else None,
                 op0=ALU.mult,
                 op1=ALU.min,
@@ -184,7 +199,11 @@ def tile_conditionaldetrspatialquerymap_x1_kernel(tc, dec, wl, bl, pq, pk, cq, c
 
         def exponentiate(i):
             nc.scalar.activation(
-                out=expz[i % 3][:], in_=neg_z[i % 3][:], func=ACT.Exp, bias=stats[i][:, 1:2], scale=-1.0,
+                out=exp_z[i % DEPTH][:],
+                in_=neg_z[i % DEPTH][:],
+                func=ACT.Exp,
+                bias=stats[i][:, 1:2],
+                scale=-1.0,
                 accum_out=stats[i][:, 2:3],
             )
 
@@ -193,269 +212,232 @@ def tile_conditionaldetrspatialquerymap_x1_kernel(tc, dec, wl, bl, pq, pk, cq, c
 
         def normalize(i, engine):
             engine.tensor_scalar(
-                out=result[i % 3][:], in0=expz[i % 3][:], scalar1=stats[i][:, 3:4], scalar2=float(N),
-                op0=ALU.mult, op1=ALU.mult,
+                out=result[i % DEPTH][:],
+                in0=exp_z[i % DEPTH][:],
+                scalar1=stats[i][:, 3:4],
+                scalar2=float(N),
+                op0=ALU.mult,
+                op1=ALU.mult,
             )
-            nc.sync.dma_start(out=out_rows[i * P : (i + 1) * P, :], in_=result[i % 3][:])
+            nc.sync.dma_start(out=out_rows[i * P : (i + 1) * P, :], in_=result[i % DEPTH][:])
 
-        def round_result(i, on_vector=True):
-            out = result16[i % 2][:].rearrange("p (g u m e) -> p g u m e", g=2, u=2, e=2)
-            in_ = result[i % 3][:].rearrange("p (g m u e) -> p g u m e", g=2, u=2, e=2)
-            if on_vector:
-                nc.vector.tensor_copy(out=out, in_=in_)
-            else:
-                nc.scalar.copy(out=out, in_=in_)
-
-        def turn_result(i, bank):
-            words = result16[i % 2][:].bitcast(F32)
-            for s in range(4):
-                nc.tensor.transpose(bank[:, s * P : (s + 1) * P], words[:, s * P : (s + 1) * P], ident[:])
-
-        def gather_result(i, bank, on_vector=False):
-            dst = plane_in[(i // 2) % 2][:, :, (i % 2) * 4 * P : (i % 2 + 1) * 4 * P].bitcast(F32)
-            out = dst.rearrange("p g (j u) -> p g j u", u=2)
-            in_ = bank[:].rearrange("p (g u j) -> p g j u", g=2, u=2)
-            if on_vector:
-                nc.vector.tensor_copy(out=out, in_=in_)
-            else:
-                nc.scalar.copy(out=out, in_=in_)
-
-        def quantize_result(c, g, lo, hi):
-            nc.vector.quantize_mx(
-                out=plane_codes[c][:, g, lo:hi].bitcast(FP8X4),
-                scales=plane_scales[c // 2][:, g, (c % 2) * ROWS + lo : (c % 2) * ROWS + hi],
-                in_=plane_in[c % 2][:, g, 4 * lo : 4 * hi],
+        def round_result(i, on_vector):
+            copy(
+                on_vector,
+                result16[i % 2][:].rearrange("p (g u m e) -> p g u m e", g=2, u=2, e=2),
+                result[i % DEPTH][:].rearrange("p (g m u e) -> p g u m e", g=2, u=2, e=2),
             )
 
-        def quantize_pair(c):
-            quantize_result(c, 0, 0, ROWS)
-            quantize_result(c, 1, 0, ROWS)
-
-        def store_words(c, lo, hi):
-            nc.sync.dma_start(
-                out=out_words[:, :, c * ROWS + lo : c * ROWS + hi], in_=plane_codes[c][:, :, lo:hi].bitcast(I32)
-            )
-
-        def store_scales(c, engines):
-            for quad in range(4):
-                engines[quad].dma_start(
-                    out=out_scales[:, 4 * quad : 4 * quad + 4, c * Q // 4 : (c + 1) * Q // 4].rearrange("g r m -> r g m"),
-                    in_=plane_scales[c][32 * quad : 32 * quad + 4].bitcast(I32),
-                )
-
-        ring = [banks[i] for i in (0, 1, 2, 3, 4, 6, 7)]
-
-        def take():
-            bank = ring.pop(0)
-            ring.append(bank)
-            return bank
-
-        held = {}
-
-        def T(name, c):
-            if name == "pq":
-                turn_pq(c, banks[5])
-            else:
-                held[name, c] = take()
-                turn(name, c, held[name, c])
-
-        def C(name, c, on_vector=False):
-            per = width[name] // ROWS
-            gather(held[name, c], grouped[name][c // per][:, (c % per) * 4 * ROWS : (c % per + 1) * 4 * ROWS], on_vector)
-
-        def Qz(name, c, chunks=1):
-            quantize(name, c, chunks)
-
-        def L(c):
-            for pair in range(2):
-                held["lam", c, pair] = take()
-                lam_matmul(c, pair, held["lam", c, pair])
-
-        def Bi(c, pair):
-            add_bias(c, pair, held["lam", c, pair])
-
-        def M(c):
-            spatial_query(c, banks[5])
-
-        def Z(i, h):
-            logits(i, h, banks[h])
-
-        def Y(i, h):
-            scale_and_max(i, h, banks[h])
-
-        def TO(i):
-            held["o", i] = take()
-            turn_result(i, held["o", i])
-
-        def I(i, on_vector=False):
-            gather_result(i, held["o", i], on_vector)
-
-        def J(i, g):
-            quantize_result(i // 2, g, (i % 2) * P, (i % 2 + 1) * P)
-
-        def Hh(i, g, engine):
-            out = result16[i % 2][:, g * HALF : (g + 1) * HALF].rearrange("p (u m e) -> p u m e", u=2, e=2)
-            in_ = result[i % 3][:, g * HALF : (g + 1) * HALF].rearrange("p (m u e) -> p u m e", u=2, e=2)
-            if engine == "v":
-                nc.vector.tensor_copy(out=out, in_=in_)
-            else:
-                nc.scalar.copy(out=out, in_=in_)
-
-        def He(i, g):
-            nc.vector.tensor_scalar(
-                out=result16[i % 2][:, g * HALF : (g + 1) * HALF].rearrange("p (u m e) -> p u m e", u=2, e=2),
-                in0=expz[i % 3][:, g * HALF : (g + 1) * HALF].rearrange("p (m u e) -> p u m e", u=2, e=2),
-                scalar1=stats[i][:, 3:4], scalar2=float(N), op0=ALU.mult, op1=ALU.mult,
-            )
-
-        def TOh(i, g):
-            held["o", i, g] = take()
-            words = result16[i % 2][:].bitcast(F32)
-            for u in range(2):
-                nc.tensor.transpose(held["o", i, g][:, u * P : (u + 1) * P], words[:, (2 * g + u) * P : (2 * g + u + 1) * P], ident[:])
-
-        def Ih(i, g):
-            dst = plane_in[(i // 2) % 2][:, g, (i % 2) * 4 * P : (i % 2 + 1) * 4 * P].bitcast(F32)
-            nc.vector.tensor_copy(
-                out=dst.rearrange("p (j u) -> p j u", u=2), in_=held["o", i, g][:, 0 : 2 * P].rearrange("p (u j) -> p j u", u=2)
-            )
-
-        def Gs(i, g):
+        def round_group(i, g, on_vector):
             cols = slice(g * HALF, (g + 1) * HALF)
-            nc.scalar.activation(out=result[i % 3][:, cols], in_=expz[i % 3][:, cols], func=ACT.Copy, scale=gain[:])
-            nc.sync.dma_start(out=out_rows[i * P : (i + 1) * P, cols], in_=result[i % 3][:, cols])
+            copy(
+                on_vector,
+                result16[i % 2][:, cols].rearrange("p (u m e) -> p u m e", u=2, e=2),
+                result[i % DEPTH][:, cols].rearrange("p (m u e) -> p u m e", u=2, e=2),
+            )
 
-        gain = sb.tile([P, 1], F32, name="gain")
+        def round_group_from_exp(i, g):
+            cols = slice(g * HALF, (g + 1) * HALF)
+            nc.vector.tensor_scalar(
+                out=result16[i % 2][:, cols].rearrange("p (u m e) -> p u m e", u=2, e=2),
+                in0=exp_z[i % DEPTH][:, cols].rearrange("p (m u e) -> p u m e", u=2, e=2),
+                scalar1=stats[i][:, 3:4],
+                scalar2=float(N),
+                op0=ALU.mult,
+                op1=ALU.mult,
+            )
 
-        def W(n):
-            for rep in range(n):
-                nc.tensor.matmul(ring[0][:, 0:P], ident[:], ident[:], start=True, stop=True)
+        def normalize_group_on_scalar(i, g):
+            cols = slice(g * HALF, (g + 1) * HALF)
+            nc.scalar.activation(
+                out=result[i % DEPTH][:, cols], in_=exp_z[i % DEPTH][:, cols], func=ACT.Copy, scale=gain[:]
+            )
+            nc.sync.dma_start(out=out_rows[i * P : (i + 1) * P, cols], in_=result[i % DEPTH][:, cols])
+
+        def turn_result(i, groups=(0, 1)):
+            bank = take_bank(("out", i, groups))
+            words = result16[i % 2][:].bitcast(F32)
+            for s in range(2 * len(groups)):
+                at = 2 * groups[0] + s
+                nc.tensor.transpose(bank[:, s * P : (s + 1) * P], words[:, at * P : (at + 1) * P], ident[:])
+
+        def gather_result(i, groups=(0, 1), on_vector=False):
+            count = len(groups)
+            dst = out_grouped[(i // 2) % 2][:, groups[0] : groups[0] + count, (i % 2) * 4 * P : (i % 2 + 1) * 4 * P]
+            copy(
+                on_vector,
+                dst.bitcast(F32).rearrange("p g (j u) -> p g j u", u=2),
+                held["out", i, groups][:, 0 : 2 * count * P].rearrange("p (g u j) -> p g j u", g=count, u=2),
+            )
+
+        def quantize_result(c, lo, hi):
+            q0 = c * ROWS % Q
+            for g in range(2):
+                nc.vector.quantize_mx(
+                    out=out_codes[c][:, g, lo:hi].bitcast(FP8X4),
+                    scales=out_bytes[c * ROWS // Q][:, g, q0 + lo : q0 + hi],
+                    in_=out_grouped[c % 2][:, g, 4 * lo : 4 * hi],
+                )
+            nc.sync.dma_start(
+                out=out_words[:, :, c * ROWS + lo : c * ROWS + hi], in_=out_codes[c][:, :, lo:hi].bitcast(I32)
+            )
+
+        def store_scales(b, queues):
+            for quad in range(4):
+                rows = out_scales[:, 4 * quad : 4 * quad + 4, b * Q // 4 : (b + 1) * Q // 4]
+                queues[quad % len(queues)].dma_start(
+                    out=rows.rearrange("g r m -> r g m"), in_=out_bytes[b][32 * quad : 32 * quad + 4].bitcast(I32)
+                )
 
         nc.sync.dma_start(out=wl_raw[:], in_=wl.rearrange("(p j) c -> p j c", j=4))
         load("dec", 0)
         nc.sync.dma_start(out=bl_raw[:], in_=bl.rearrange("(p t) -> p t", t=4))
-        for name, c in (("pk", 0), ("ck", 0), ("pq", 0), ("dec", 1), ("pk", 1), ("ck", 1), ("cq", 0), ("pk", 2), ("ck", 2), ("pq", 1), ("pk", 3), ("ck", 3), ("cq", 1), ("dec", 2), ("ck", 4), ("ck", 5), ("pq", 2), ("cq", 2), ("dec", 3), ("ck", 6), ("ck", 7), ("pq", 3), ("cq", 3)):
+        first_chunks = (
+            ("pk", 0), ("ck", 0), ("pq", 0), ("dec", 1), ("pk", 1), ("ck", 1), ("cq", 0),
+            ("pk", 2), ("ck", 2), ("pq", 1), ("pk", 3), ("ck", 3), ("cq", 1), ("dec", 2),
+        )
+        for name, c in first_chunks + LATER_CHUNKS:
             load(name, c)
         nc.scalar.activation(out=bl_f32[:], in_=bl_raw[:], func=ACT.Identity)
 
-        W(W0)
+        warm_up(WARM_AT_START)
         group_wl()
-        T("dec", 0); C("dec", 0)
-        quantize_wl()
-        T("pk", 0); C("pk", 0)
-        Qz("dec", 0)
-        W(W1)
-        T("ck", 0)
-        Qz("pk", 0)
-        C("ck", 0, True)
-        L(0)
-        T("pq", 0)
-        Bi(0, 0); Bi(0, 1)
-        Qz("ck", 0)
-        T("dec", 1); C("dec", 1)
-        T("pk", 1); C("pk", 1)
-        ring.remove(banks[0])
-        W(W2)
-        M(0)
-        T("ck", 1); C("ck", 1)
-        T("cq", 0); C("cq", 0)
-        Qz("dec", 1); Qz("sq", 0); Qz("pk", 1); Qz("ck", 1)
-        T("pk", 2); C("pk", 2)
-        ring.remove(banks[1])
-        L(1)
-        Bi(1, 0); Bi(1, 1)
-        Qz("cq", 0)
-        Qz("pk", 2)
-        T("ck", 2); C("ck", 2, True)
-        T("pq", 1)
-        T("pk", 3); C("pk", 3)
-        T("ck", 3); C("ck", 3)
-        Z(0, 0)
-        T("cq", 1); C("cq", 1)
-        T("dec", 2); C("dec", 2)
-        M(1)
-        Qz("ck", 2)
-        Qz("pk", 3)
-        Qz("ck", 3)
-        Y(0, 0)
-        Qz("sq", 1)
+        turn("dec", 0)
+        gather("dec", 0)
+        nc.vector.quantize_mx(out=wl_codes[:].bitcast(FP8X4), scales=wl_scales[:], in_=wl_grouped[:])
+        turn("pk", 0)
+        gather("pk", 0)
+        quantize("dec", 0)
+        warm_up(WARM_BEFORE_LAM)
+        turn("ck", 0)
+        quantize("pk", 0)
+        gather("ck", 0, on_vector=True)
+        lam_product(0)
+        turn("pq", 0)
+        add_bias(0)
+        quantize("ck", 0)
+        turn("dec", 1)
+        gather("dec", 1)
+        turn("pk", 1)
+        gather("pk", 1)
+        rotation.remove(logit_banks[0])
+        warm_up(1)
+        spatial_query(0)
+        turn("ck", 1)
+        gather("ck", 1)
+        turn("cq", 0)
+        gather("cq", 0)
+        for name, c in (("dec", 1), ("sq", 0), ("pk", 1), ("ck", 1)):
+            quantize(name, c)
+        turn("pk", 2)
+        gather("pk", 2)
+        rotation.remove(logit_banks[1])
+        lam_product(1)
+        add_bias(1)
+        quantize("cq", 0)
+        quantize("pk", 2)
+        turn("ck", 2)
+        gather("ck", 2, on_vector=True)
+        turn("pq", 1)
+        warm_up(1)
+        for name in ("pk", "ck"):
+            turn(name, 3)
+            gather(name, 3)
+        logits(0, 0)
+        for name, c in (("cq", 1), ("dec", 2)):
+            turn(name, c)
+            gather(name, c)
+        spatial_query(1)
+        for name, c in (("ck", 2), ("pk", 3), ("ck", 3)):
+            quantize(name, c)
+        scale_and_max(0, 0)
+        quantize("sq", 1)
 
-        LAST = TILES - 1
+        waiting = list(LATER_CHUNKS)
+        carried = None
+        ready = [("cq", 1), ("dec", 2)]
         for i in range(LAST):
-            k = i // 2 + 1 if i % 2 == 0 and i < 6 else None
-            Z(i, 1)
-            Z(i + 1, 0)
-            if i in (1, 3):
-                L(i // 2 + 2)
+            turned = [waiting.pop(0) for repeat in range(TURNS_PER_STEP[i])] if i < len(TURNS_PER_STEP) else []
+            copied_now = [chunk for chunk in turned[:-1] if chunk[0] != "pq"]
+            lam_chunk = (i + 3) // 2 if i % 2 == 1 and (i + 3) // 2 < CHUNKS else None
+            sq_chunk = (i + 2) // 2 if i % 2 == 0 and 2 <= (i + 2) // 2 < CHUNKS else None
+
+            logits(i, 1)
+            logits(i + 1, 0)
+            if lam_chunk:
+                lam_product(lam_chunk)
             if i >= 1:
                 invert_sum(i - 1)
-            for name, c in first.get(i, []):
-                T(name, c)
-            for name, c in early.get(i, []):
-                C(name, c)
-            Y(i, 1)
+                normalize(i - 1, nc.gpsimd)
+            if carried:
+                gather(*carried)
+                ready.append(carried)
+            scale_and_max(i, 1)
             exponentiate(i)
-            if i >= 1:
-                normalize(i - 1, nc.vector)
-            for name, c, n in mid.get(i, []):
-                Qz(name, c, n)
-            Y(i + 1, 0)
-            if i in (1, 3):
-                Bi(i // 2 + 2, 0); Bi(i // 2 + 2, 1)
-            for name, c in turns.get(i, [])[:TN.get(i, 0)]:
-                T(name, c)
-            if 2 <= i:
-                TO(i - 2)
-            for name, c in turns.get(i, [])[TN.get(i, 0):]:
-                T(name, c)
-            if k and i:
-                M(k)
-            for name, c in late.get(i, [])[:CN.get(i, 1)]:
-                C(name, c)
-            if i in HS:
-                Hh(i - 1, 1, "s")
-            if i in HF:
-                round_result(i - 1, False)
-            if 2 <= i:
-                I(i - 2)
-            for name, c in late.get(i, [])[CN.get(i, 1):]:
-                C(name, c)
-            for name, c, n in quants.get(i, []):
-                Qz(name, c, n)
-            if k and i:
-                Qz("sq", k)
-            if i in JJ:
-                quantize_pair(JJ[i])
-            if i in HS:
-                Hh(i - 1, 0, "v")
-            elif i >= 1 and i not in HF:
-                round_result(i - 1)
-            for name, c, n in quants_late.get(i, []):
-                Qz(name, c, n)
-            if i in JJ:
-                store_words(JJ[i], 0, ROWS)
-                if JJ[i] == 1:
-                    store_scales(0, [nc.sync] * 4)
+            scale_and_max(i + 1, 0)
+            if lam_chunk:
+                add_bias(lam_chunk)
+            for chunk in copied_now:
+                turn(*chunk)
+            if i >= 2:
+                turn_result(i - 2)
+            for chunk in turned:
+                if chunk not in copied_now:
+                    turn(*chunk)
+            if sq_chunk:
+                spatial_query(sq_chunk)
+            for chunk in copied_now:
+                gather(*chunk)
+            if i == SCALAR_ROUNDS:
+                round_result(i - 1, on_vector=False)
+            if i > SCALAR_ROUNDS:
+                round_group(i - 1, 1, on_vector=False)
+            if i >= 2:
+                gather_result(i - 2)
 
-        Z(7, 1)
-        TO(5)
-        invert_sum(6)
-        I(5)
-        Y(7, 1)
-        exponentiate(7)
-        He(6, 0); He(6, 1)
-        normalize(6, nc.vector)
-        TO(6); I(6)
-        quantize_pair(2)
-        store_words(2, 0, ROWS)
-        invert_sum(7)
-        nc.vector.tensor_scalar(out=gain[:], in0=stats[7][:, 3:4], scalar1=float(N), scalar2=None, op0=ALU.mult)
-        He(7, 0); He(7, 1)
-        Gs(7, 0); Gs(7, 1)
-        TOh(7, 0); TOh(7, 1)
-        J(6, 0); J(6, 1)
-        store_words(3, 0, P)
-        Ih(7, 0); Ih(7, 1)
-        J(7, 0); J(7, 1)
-        store_words(3, P, ROWS)
-        store_scales(1, [nc.scalar, nc.sync, nc.scalar, nc.sync])
+            for name, c in ready:
+                if name == "cq":
+                    quantize(name, c)
+                if name == "ck":
+                    quantize(name, c - 1, chunks=2)
+            if sq_chunk:
+                quantize("sq", sq_chunk)
+            if i >= 4 and i % 2 == 0:
+                quantize_result(i // 2 - 2, 0, ROWS)
+            if i == LAST - 1:
+                store_scales(0, [nc.sync])
+            if 1 <= i < SCALAR_ROUNDS:
+                round_result(i - 1, on_vector=True)
+            if i > SCALAR_ROUNDS:
+                round_group(i - 1, 0, on_vector=True)
+            for name, c in ready + copied_now:
+                if name == "dec":
+                    quantize(name, c)
+            ready = []
+            carried = turned[-1] if turned else None
+
+        logits(LAST, 1)
+        turn_result(LAST - 2)
+        invert_sum(LAST - 1)
+        gather_result(LAST - 2)
+        scale_and_max(LAST, 1)
+        exponentiate(LAST)
+        for g in range(2):
+            round_group_from_exp(LAST - 1, g)
+        normalize(LAST - 1, nc.vector)
+        turn_result(LAST - 1)
+        gather_result(LAST - 1)
+        quantize_result(CHUNKS - 2, 0, ROWS)
+        invert_sum(LAST)
+        nc.vector.tensor_scalar(out=gain[:], in0=stats[LAST][:, 3:4], scalar1=float(N), scalar2=None, op0=ALU.mult)
+        for g in range(2):
+            round_group_from_exp(LAST, g)
+        for g in range(2):
+            normalize_group_on_scalar(LAST, g)
+        for g in range(2):
+            turn_result(LAST, (g,))
+        quantize_result(CHUNKS - 1, 0, P)
+        for g in range(2):
+            gather_result(LAST, (g,), on_vector=True)
+        quantize_result(CHUNKS - 1, P, ROWS)
+        store_scales(1, [nc.scalar, nc.sync])

from contextlib import ExitStack

import concourse.mybir as mybir
from concourse.masks import make_identity

B, Q, N, D = 2, 512, 1024, 512
FLOPS = 2 * B * Q * D * D + 2 * 2 * B * Q * N * D

F32 = mybir.dt.float32
BF16 = mybir.dt.bfloat16
U32 = mybir.dt.uint32
I32 = mybir.dt.int32
U8 = mybir.dt.uint8
FP8X4 = mybir.dt.float8_e4m3fn_x4
ALU = mybir.AluOpType
ACT = mybir.ActivationFunctionType

P = 128
ROWS = 256
HALF = 512
CHUNKS = B * Q // ROWS
TILES = B * Q // P
LAST = TILES - 1
DEPTH = 3
LOGIT_SCALE = 1.0 / 32.0

WARM_AT_START = 7
WARM_BEFORE_LAM = 2

LATER_CHUNKS = (("ck", 4), ("ck", 5), ("pq", 2), ("cq", 2), ("dec", 3), ("ck", 6), ("ck", 7), ("pq", 3), ("cq", 3))
TURNS_PER_STEP = (2, 2, 3, 2)
SCALAR_ROUNDS = len(TURNS_PER_STEP)


def tile_conditionaldetrspatialquerymap_x1_kernel(tc, dec, wl, bl, pq, pk, cq, ck, out_0, out_1, out_2):
    nc = tc.nc
    with ExitStack() as ctx:
        sb = ctx.enter_context(tc.tile_pool(name="sb", bufs=1))
        ps = ctx.enter_context(tc.psum_pool(name="ps", bufs=1))
        ctx.enter_context(tc.manual_schedule())

        def tiles(name, count, shape, dtype):
            return [sb.tile(shape, dtype, name="%s%d" % (name, i), align_bytes=64) for i in range(count)]

        banks = [ps.tile([P, HALF], F32, name="bank%d" % i) for i in range(8)]
        ident = sb.tile([P, P], F32, name="ident")
        make_identity(nc, ident[:])

        source = {
            "dec": dec.rearrange("b q k -> (b q) k"),
            "pq": pq.rearrange("b q k -> (b q) k"),
            "cq": cq.rearrange("b q k -> (b q) k"),
            "ck": ck.rearrange("b n k -> (b n) k"),
            "pk": pk,
        }
        out_rows = out_0.rearrange("b q n -> (b q) n")
        out_words = out_1.rearrange("g p m t -> p g (m t)").bitcast(I32)
        out_scales = out_2.bitcast(I32)

        raw = {name: tiles(name + "_raw", source[name].shape[0] // ROWS, [P, 2, D], BF16) for name in source}
        width = {"dec": ROWS, "cq": ROWS, "sq": ROWS, "ck": HALF, "pk": HALF}
        operands = {"dec": CHUNKS, "cq": CHUNKS, "sq": CHUNKS, "ck": B * N // HALF, "pk": N // HALF}
        codes = {name: tiles(name + "_codes", operands[name], [P, width[name]], U32) for name in width}
        scales = {name: tiles(name + "_scales", operands[name], [P, width[name]], U8) for name in width}
        grouped = {name: tiles(name + "_grouped", operands[name], [P, 4 * width[name]], BF16) for name in width}
        wl_raw = sb.tile([P, 4, D], BF16, name="wl_raw")
        wl_grouped = sb.tile([P, 4 * D], BF16, name="wl_grouped", align_bytes=64)
        wl_codes = sb.tile([P, D], U32, name="wl_codes", align_bytes=64)
        wl_scales = sb.tile([P, D], U8, name="wl_scales", align_bytes=64)
        bl_raw = sb.tile([P, 4], BF16, name="bl_raw")
        bl_f32 = sb.tile([P, 4], F32, name="bl_f32")
        lam = tiles("lam", 2, [P, 4 * ROWS], F32)
        neg_z = tiles("neg_z", DEPTH, [P, N], F32)
        exp_z = tiles("exp_z", DEPTH, [P, N], F32)
        result = tiles("result", DEPTH, [P, N], F32)
        result16 = tiles("result16", 2, [P, N], BF16)
        stats = tiles("stats", TILES, [P, 4], F32)
        out_grouped = tiles("out_grouped", 2, [P, 2, 4 * ROWS], BF16)
        out_codes = tiles("out_codes", CHUNKS, [P, 2, ROWS], U32)
        out_bytes = tiles("out_bytes", B, [P, 2, Q], U8)
        warm = sb.tile([P, P], F32, name="warm")
        nc.vector.memset(warm[:], 0.0)
        gain = sb.tile([P, 1], F32, name="gain")

        logit_banks = banks[0:2]
        pq_bank = banks[5]
        rotation = banks[0:5] + banks[6:8]
        held = {}

        def take_bank(key):
            held[key] = rotation.pop(0)
            rotation.append(held[key])
            return held[key]

        def warm_up(count):
            for repeat in range(count):
                nc.tensor.matmul(rotation[0][:, 0:P], warm[:], warm[:], start=True, stop=True)

        def load(name, c):
            rows = source[name][c * ROWS : (c + 1) * ROWS, :]
            order = "(r p) k -> p r k" if name == "pq" else "(p r) k -> p r k"
            nc.sync.dma_start(out=raw[name][c][:], in_=rows.rearrange(order, r=2))

        def turn(name, c):
            if name == "pq":
                slots = pq_bank[:].rearrange("p (r c u i) -> p r u c i", r=2, u=2, i=4)
            else:
                slots = take_bank((name, c))[:].rearrange("p (r u j) -> p r u j", r=2, u=2)
            for r in range(2):
                words = raw[name][c][:, r, :].bitcast(F32)
                for u in range(2):
                    nc.tensor.transpose(slots[:, r, u], words[:, u : D // 2 : 2], ident[:])

        def copy(on_vector, out, in_):
            if on_vector:
                nc.vector.tensor_copy(out=out, in_=in_)
            else:
                nc.scalar.copy(out=out, in_=in_)

        def gather(name, c, on_vector=False):
            per = width[name] // ROWS
            dst = grouped[name][c // per][:, (c % per) * 4 * ROWS : (c % per + 1) * 4 * ROWS].bitcast(F32)
            copy(
                on_vector,
                dst.rearrange("p (j r u) -> p j r u", r=2, u=2),
                held[name, c][:].rearrange("p (r u j) -> p j r u", r=2, u=2),
            )

        def quantize(name, c, chunks=1):
            per = width[name] // ROWS
            lo, hi = (c % per) * ROWS, (c % per + chunks) * ROWS
            nc.vector.quantize_mx(
                out=codes[name][c // per][:, lo:hi].bitcast(FP8X4),
                scales=scales[name][c // per][:, lo:hi],
                in_=grouped[name][c // per][:, 4 * lo : 4 * hi],
            )

        def group_wl():
            nc.vector.tensor_copy(
                out=wl_grouped[:].rearrange("p (t c i j) -> p c t i j", t=4, i=2, j=4),
                in_=wl_raw[:].rearrange("p j (c i t) -> p c t i j", i=2, t=4),
            )

        def lam_product(c):
            for t in range(4):
                bank = held["lam", t // 2] if t % 2 else take_bank(("lam", t // 2))
                nc.tensor.matmul_mx(
                    out=bank[:, (t % 2) * ROWS : (t % 2 + 1) * ROWS],
                    lhsT=wl_codes[:, t * P : (t + 1) * P].bitcast(FP8X4),
                    lhsT_scale=wl_scales[:, t * P : (t + 1) * P],
                    rhs=codes["dec"][c][:].bitcast(FP8X4),
                    rhs_scale=scales["dec"][c][:],
                    start=True,
                    stop=True,
                )

        def add_bias(c):
            slots = lam[c % 2][:].rearrange("p (c t i) -> p t c i", t=4, i=4)
            for t in range(4):
                nc.scalar.activation(
                    out=slots[:, t],
                    in_=held["lam", t // 2][:, (t % 2) * ROWS : (t % 2 + 1) * ROWS].rearrange("p (c i) -> p c i", i=4),
                    func=ACT.Identity,
                    bias=bl_f32[:, t : t + 1],
                )

        def spatial_query(c):
            nc.vector.tensor_tensor(
                out=grouped["sq"][c][:].rearrange("p (c i u e) -> p c u e i", i=4, u=2, e=2),
                in0=lam[c % 2][:].rearrange("p (c u e i) -> p c u e i", u=2, e=2, i=4),
                in1=pq_bank[:].bitcast(BF16).rearrange("p (c u i e) -> p c u e i", u=2, i=4, e=2),
                op=ALU.mult,
            )

        def logits(i, h):
            c, cols = i // 2, slice((i % 2) * P, (i % 2 + 1) * P)
            b = i * P // Q
            for first, query, key, k in ((True, "cq", "ck", 2 * b + h), (False, "sq", "pk", h)):
                nc.tensor.matmul_mx(
                    out=logit_banks[h][:],
                    lhsT=codes[query][c][:, cols].bitcast(FP8X4),
                    lhsT_scale=scales[query][c][:, cols],
                    rhs=codes[key][k][:].bitcast(FP8X4),
                    rhs_scale=scales[key][k][:],
                    start=first,
                    stop=not first,
                )

        def scale_and_max(i, h):
            nc.vector.tensor_scalar(
                out=neg_z[i % DEPTH][:, h * HALF : (h + 1) * HALF],
                in0=logit_banks[h][:],
                scalar1=-LOGIT_SCALE,
                scalar2=stats[i][:, 0:1] if h else None,
                op0=ALU.mult,
                op1=ALU.min,
                accum_out=stats[i][:, h : h + 1],
            )

        def exponentiate(i):
            nc.scalar.activation(
                out=exp_z[i % DEPTH][:],
                in_=neg_z[i % DEPTH][:],
                func=ACT.Exp,
                bias=stats[i][:, 1:2],
                scale=-1.0,
                accum_out=stats[i][:, 2:3],
            )

        def invert_sum(i):
            nc.vector.reciprocal(out=stats[i][:, 3:4], in_=stats[i][:, 2:3])

        def normalize(i, engine):
            engine.tensor_scalar(
                out=result[i % DEPTH][:],
                in0=exp_z[i % DEPTH][:],
                scalar1=stats[i][:, 3:4],
                scalar2=float(N),
                op0=ALU.mult,
                op1=ALU.mult,
            )
            nc.sync.dma_start(out=out_rows[i * P : (i + 1) * P, :], in_=result[i % DEPTH][:])

        def round_result(i, on_vector):
            copy(
                on_vector,
                result16[i % 2][:].rearrange("p (g u m e) -> p g u m e", g=2, u=2, e=2),
                result[i % DEPTH][:].rearrange("p (g m u e) -> p g u m e", g=2, u=2, e=2),
            )

        def round_group(i, g, on_vector):
            cols = slice(g * HALF, (g + 1) * HALF)
            copy(
                on_vector,
                result16[i % 2][:, cols].rearrange("p (u m e) -> p u m e", u=2, e=2),
                result[i % DEPTH][:, cols].rearrange("p (m u e) -> p u m e", u=2, e=2),
            )

        def round_group_from_exp(i, g):
            cols = slice(g * HALF, (g + 1) * HALF)
            nc.vector.tensor_scalar(
                out=result16[i % 2][:, cols].rearrange("p (u m e) -> p u m e", u=2, e=2),
                in0=exp_z[i % DEPTH][:, cols].rearrange("p (m u e) -> p u m e", u=2, e=2),
                scalar1=stats[i][:, 3:4],
                scalar2=float(N),
                op0=ALU.mult,
                op1=ALU.mult,
            )

        def normalize_group_on_scalar(i, g):
            cols = slice(g * HALF, (g + 1) * HALF)
            nc.scalar.activation(
                out=result[i % DEPTH][:, cols], in_=exp_z[i % DEPTH][:, cols], func=ACT.Copy, scale=gain[:]
            )
            nc.sync.dma_start(out=out_rows[i * P : (i + 1) * P, cols], in_=result[i % DEPTH][:, cols])

        def turn_result(i, groups=(0, 1)):
            bank = take_bank(("out", i, groups))
            words = result16[i % 2][:].bitcast(F32)
            for s in range(2 * len(groups)):
                at = 2 * groups[0] + s
                nc.tensor.transpose(bank[:, s * P : (s + 1) * P], words[:, at * P : (at + 1) * P], ident[:])

        def gather_result(i, groups=(0, 1), on_vector=False):
            count = len(groups)
            dst = out_grouped[(i // 2) % 2][:, groups[0] : groups[0] + count, (i % 2) * 4 * P : (i % 2 + 1) * 4 * P]
            copy(
                on_vector,
                dst.bitcast(F32).rearrange("p g (j u) -> p g j u", u=2),
                held["out", i, groups][:, 0 : 2 * count * P].rearrange("p (g u j) -> p g j u", g=count, u=2),
            )

        def quantize_result(c, lo, hi):
            q0 = c * ROWS % Q
            for g in range(2):
                nc.vector.quantize_mx(
                    out=out_codes[c][:, g, lo:hi].bitcast(FP8X4),
                    scales=out_bytes[c * ROWS // Q][:, g, q0 + lo : q0 + hi],
                    in_=out_grouped[c % 2][:, g, 4 * lo : 4 * hi],
                )
            nc.sync.dma_start(
                out=out_words[:, :, c * ROWS + lo : c * ROWS + hi], in_=out_codes[c][:, :, lo:hi].bitcast(I32)
            )

        def store_scales(b, queues):
            for quad in range(4):
                rows = out_scales[:, 4 * quad : 4 * quad + 4, b * Q // 4 : (b + 1) * Q // 4]
                queues[quad % len(queues)].dma_start(
                    out=rows.rearrange("g r m -> r g m"), in_=out_bytes[b][32 * quad : 32 * quad + 4].bitcast(I32)
                )

        nc.sync.dma_start(out=wl_raw[:], in_=wl.rearrange("(p j) c -> p j c", j=4))
        load("dec", 0)
        nc.sync.dma_start(out=bl_raw[:], in_=bl.rearrange("(p t) -> p t", t=4))
        first_chunks = (
            ("pk", 0), ("ck", 0), ("pq", 0), ("dec", 1), ("pk", 1), ("ck", 1), ("cq", 0),
            ("pk", 2), ("ck", 2), ("pq", 1), ("pk", 3), ("ck", 3), ("cq", 1), ("dec", 2),
        )
        for name, c in first_chunks + LATER_CHUNKS:
            load(name, c)
        nc.scalar.activation(out=bl_f32[:], in_=bl_raw[:], func=ACT.Identity)

        warm_up(WARM_AT_START)
        group_wl()
        turn("dec", 0)
        gather("dec", 0)
        nc.vector.quantize_mx(out=wl_codes[:].bitcast(FP8X4), scales=wl_scales[:], in_=wl_grouped[:])
        turn("pk", 0)
        gather("pk", 0)
        quantize("dec", 0)
        warm_up(WARM_BEFORE_LAM)
        turn("ck", 0)
        quantize("pk", 0)
        gather("ck", 0, on_vector=True)
        lam_product(0)
        turn("pq", 0)
        add_bias(0)
        quantize("ck", 0)
        turn("dec", 1)
        gather("dec", 1)
        turn("pk", 1)
        gather("pk", 1)
        rotation.remove(logit_banks[0])
        warm_up(1)
        spatial_query(0)
        turn("ck", 1)
        gather("ck", 1)
        turn("cq", 0)
        gather("cq", 0)
        for name, c in (("dec", 1), ("sq", 0), ("pk", 1), ("ck", 1)):
            quantize(name, c)
        turn("pk", 2)
        gather("pk", 2)
        rotation.remove(logit_banks[1])
        lam_product(1)
        add_bias(1)
        quantize("cq", 0)
        quantize("pk", 2)
        turn("ck", 2)
        gather("ck", 2, on_vector=True)
        turn("pq", 1)
        warm_up(1)
        for name in ("pk", "ck"):
            turn(name, 3)
            gather(name, 3)
        logits(0, 0)
        for name, c in (("cq", 1), ("dec", 2)):
            turn(name, c)
            gather(name, c)
        spatial_query(1)
        for name, c in (("ck", 2), ("pk", 3), ("ck", 3)):
            quantize(name, c)
        scale_and_max(0, 0)
        quantize("sq", 1)

        waiting = list(LATER_CHUNKS)
        carried = None
        ready = [("cq", 1), ("dec", 2)]
        for i in range(LAST):
            turned = [waiting.pop(0) for repeat in range(TURNS_PER_STEP[i])] if i < len(TURNS_PER_STEP) else []
            copied_now = [chunk for chunk in turned[:-1] if chunk[0] != "pq"]
            lam_chunk = (i + 3) // 2 if i % 2 == 1 and (i + 3) // 2 < CHUNKS else None
            sq_chunk = (i + 2) // 2 if i % 2 == 0 and 2 <= (i + 2) // 2 < CHUNKS else None

            logits(i, 1)
            logits(i + 1, 0)
            if lam_chunk:
                lam_product(lam_chunk)
            if i >= 1:
                invert_sum(i - 1)
                normalize(i - 1, nc.gpsimd)
            if carried:
                gather(*carried)
                ready.append(carried)
            scale_and_max(i, 1)
            exponentiate(i)
            scale_and_max(i + 1, 0)
            if lam_chunk:
                add_bias(lam_chunk)
            for chunk in copied_now:
                turn(*chunk)
            if i >= 2:
                turn_result(i - 2)
            for chunk in turned:
                if chunk not in copied_now:
                    turn(*chunk)
            if sq_chunk:
                spatial_query(sq_chunk)
            for chunk in copied_now:
                gather(*chunk)
            if i == SCALAR_ROUNDS:
                round_result(i - 1, on_vector=False)
            if i > SCALAR_ROUNDS:
                round_group(i - 1, 1, on_vector=False)
            if i >= 2:
                gather_result(i - 2)

            for name, c in ready:
                if name == "cq":
                    quantize(name, c)
                if name == "ck":
                    quantize(name, c - 1, chunks=2)
            if sq_chunk:
                quantize("sq", sq_chunk)
            if i >= 4 and i % 2 == 0:
                quantize_result(i // 2 - 2, 0, ROWS)
            if i == LAST - 1:
                store_scales(0, [nc.sync])
            if 1 <= i < SCALAR_ROUNDS:
                round_result(i - 1, on_vector=True)
            if i > SCALAR_ROUNDS:
                round_group(i - 1, 0, on_vector=True)
            for name, c in ready + copied_now:
                if name == "dec":
                    quantize(name, c)
            ready = []
            carried = turned[-1] if turned else None

        logits(LAST, 1)
        turn_result(LAST - 2)
        invert_sum(LAST - 1)
        gather_result(LAST - 2)
        scale_and_max(LAST, 1)
        exponentiate(LAST)
        for g in range(2):
            round_group_from_exp(LAST - 1, g)
        normalize(LAST - 1, nc.vector)
        turn_result(LAST - 1)
        gather_result(LAST - 1)
        quantize_result(CHUNKS - 2, 0, ROWS)
        invert_sum(LAST)
        nc.vector.tensor_scalar(out=gain[:], in0=stats[LAST][:, 3:4], scalar1=float(N), scalar2=None, op0=ALU.mult)
        for g in range(2):
            round_group_from_exp(LAST, g)
        for g in range(2):
            normalize_group_on_scalar(LAST, g)
        for g in range(2):
            turn_result(LAST, (g,))
        quantize_result(CHUNKS - 1, 0, P)
        for g in range(2):
            gather_result(LAST, (g,), on_vector=True)
        quantize_result(CHUNKS - 1, P, ROWS)
        store_scales(1, [nc.scalar, nc.sync])
